import numpy as np
import ml_dtypes


def mxq(x, axis, fmt="e4m3"):
    dtype, down = {"e4m3": (ml_dtypes.float8_e4m3fn, 7), "e5m2": (ml_dtypes.float8_e5m2, 14)}[fmt]
    v = np.moveaxis(np.asarray(x, np.float32).astype(ml_dtypes.bfloat16).astype(np.float64), axis, -1)
    blocks = v.reshape(v.shape[:-1] + (-1, 32))
    amax = np.abs(blocks).max(-1, keepdims=True)
    byte = np.maximum(np.where(amax > 0, np.frexp(amax)[1] - 1 + 127, 0) - down, 1)
    scale = np.exp2(byte - 127.0)
    codes = (blocks / scale).astype(np.float32).astype(dtype).astype(np.float64)
    return np.moveaxis((codes * scale).reshape(v.shape), -1, axis)


WIDE = False


def mx_kscale(k):
    if not WIDE:
        return np.ones(k)
    levels = np.array([10, -10, 5, -5, 0])
    if k % 512:
        return np.exp2(np.random.permutation(np.resize(levels, k // 32))).repeat(32)
    a = np.empty((k // 512, 16))
    for p in range(k // 512):
        a[p, :8] = np.random.permutation(np.resize(levels, 8))
        for g in range(8):
            far = levels[np.abs(levels - a[p, g]) >= 10]
            a[p, g + 8] = far[np.random.randint(len(far))]
    return np.exp2(a.ravel()).repeat(32)


def f64(x):
    return np.asarray(x).astype(np.float64)


def striped(idx):
    return np.tile(idx.reshape(-1, 16).T, (8, 1)).astype(np.uint16)


def unstriped(offs):
    return offs[:16].T.reshape(-1).astype(np.int64)


def pack_weight(w):
    k, n = w.shape
    w = f64(np.asarray(w, np.float32).astype(ml_dtypes.bfloat16)).reshape(k // 32, 32, n)
    amax = np.abs(w).max(1)
    byte = np.clip(np.where(amax > 0, np.frexp(amax)[1] - 1 + 127 - 7, 1), 1, 254)
    scaled = (w * np.exp2(127.0 - byte)[:, None, :]).reshape(k, n).astype(np.float32)
    words = np.ascontiguousarray(scaled.reshape(k // 512, 128, 4, n).transpose(0, 1, 3, 2)).astype(ml_dtypes.float8_e4m3fn).view(np.uint8)
    return words, np.ascontiguousarray(byte.astype(np.uint8).reshape(k // 512, 16, n))


def unpack_weight(words, scales):
    g, p, n, _ = words.shape
    vals = np.ascontiguousarray(words).view(ml_dtypes.float8_e4m3fn).astype(np.float64) * np.repeat(np.exp2(scales.astype(np.float64) - 127.0), 8, axis=1)[..., None]
    return vals.transpose(0, 1, 3, 2).reshape(g * 512, n)


E2M1 = np.array([0.0, 0.5, 1.0, 1.5, 2.0, 3.0, 4.0, 6.0, -0.0, -0.5, -1.0, -1.5, -2.0, -3.0, -4.0, -6.0])


def pack_fp4(w):
    k, n = w.shape
    w = f64(np.asarray(w, np.float32).astype(ml_dtypes.bfloat16)).reshape(k // 32, 32, n)
    amax = np.abs(w).max(1)
    mant, ex = np.frexp(amax / 6.0)
    byte = np.clip(np.where(amax > 0, np.where(mant > 0.5, ex, ex - 1) + 127, 1), 1, 254)
    scaled = (w * np.exp2(127.0 - byte)[:, None, :]).reshape(k, n).astype(np.float32)
    c = np.ascontiguousarray(scaled.reshape(k // 512, 128, 4, n).transpose(0, 1, 3, 2)).astype(ml_dtypes.float4_e2m1fn).view(np.uint8) & 0xF
    words = (c[..., 0::2] | (c[..., 1::2] << 4)).reshape(k // 512, 128, 2 * n)
    return np.ascontiguousarray(words), np.ascontiguousarray(byte.astype(np.uint8).reshape(k // 512, 16, n))


def unpack_fp4(words, scales):
    g, _, n = scales.shape
    words = np.ascontiguousarray(words).reshape(g, 128, n, 2)
    nib = np.empty((g, 128, n, 4), np.uint8)
    nib[..., 0::2] = words & 0xF
    nib[..., 1::2] = words >> 4
    vals = E2M1[nib] * np.repeat(np.exp2(scales.astype(np.float64) - 127.0), 8, axis=1)[..., None]
    return vals.transpose(0, 1, 3, 2).reshape(g * 512, n)


def planes(y):
    n, m = y.shape
    v = y.astype(np.float32).astype(ml_dtypes.bfloat16).astype(np.float64).reshape(n // 32, 32, m)
    top = np.abs(v).max(1)
    byte = np.clip(np.where(top > 0, np.frexp(top)[1] - 1 + 127 - 7, 1), 1, 254)
    codes = (v * np.exp2(127.0 - byte)[:, None, :]).reshape(n, m).astype(np.float32).astype(ml_dtypes.float8_e4m3fn).view(np.uint8)
    words = codes.reshape(n // 512, 128, 4, m).transpose(0, 1, 3, 2)
    return np.ascontiguousarray(words), np.ascontiguousarray(byte.astype(np.uint8).reshape(n // 512, 16, m))


def relu(v):
    return np.maximum(v, 0.0)


K, T, S, H, N = 1024, 1024, 512, 512, 512


def setup_inputs():
    n = np.random.standard_normal
    s = mx_kscale(K)[:, None]
    u = mx_kscale(H)
    packed_xT = pack_weight(n((K, T)) * s)
    packed_w2 = pack_fp4(n((H, N)) / np.sqrt(H) / u[:, None])
    return {
        "x_words": packed_xT[0],
        "x_scales": packed_xT[1],
        "mask": (n((N, T))).astype(np.float32),
        "w1": (n((K, H)) / np.sqrt(K) / s * u).astype(np.float32),
        "w2_words": packed_w2[0],
        "w2_scales": packed_w2[1],
        "offs": striped(np.random.permutation(T)[:S]),
    }


def reference(x_words, x_scales, mask, w1, w2_words, w2_scales, offs):
    xq = unpack_weight(x_words, x_scales)[:, unstriped(offs)]
    h = relu(mxq(f64(w1), 0, "e4m3").T @ xq)
    y = unpack_fp4(w2_words, w2_scales).T @ mxq(h, 0, "e4m3")
    out = f64(mask).copy()
    out[:, unstriped(offs)] = y
    out_0 = out
    return (out_0,) + planes(out_0)

@@ -1,0 +1,210 @@
+from contextlib import ExitStack
+
+import concourse.mybir as mybir
+
+K, T, S, H, N = 1024, 1024, 512, 512, 512
+FLOPS = 2 * K * H * S + 2 * H * N * S
+
+F32 = mybir.dt.float32
+BF16 = mybir.dt.bfloat16
+I32 = mybir.dt.int32
+U32 = mybir.dt.uint32
+U16 = mybir.dt.uint16
+U8 = mybir.dt.uint8
+FP8X4 = mybir.dt.float8_e4m3fn_x4
+FP4X4 = mybir.dt.float4_e2m1fn_x4
+RELU = mybir.ActivationFunctionType.Relu
+COPY = mybir.ActivationFunctionType.Copy
+
+P = 128
+PACK = 4
+PASSES = K // (P * PACK)
+CHUNK = 128
+CHUNKS = S // CHUNK
+HALF = T // 2
+SCALAR_SHARE = (96, 48)
+
+
+def tile_picked_zmae_mlprelu_po_kernel(
+    tc, x_words, x_scales, mask, w1, w2_words, w2_scales, offs, out_0, out_1, out_2
+):
+    nc = tc.nc
+    with ExitStack() as ctx:
+        keep = ctx.enter_context(tc.tile_pool(name="keep", bufs=1))
+        psum = ctx.enter_context(tc.psum_pool(name="psum", bufs=1))
+
+        def sb(name, shape, dtype, tag=""):
+            return keep.tile(shape, dtype, name=name, tag=tag or name, align_bytes=64)
+
+        offsets = sb("offsets", [P, S // 16], U16)
+        nc.sync.dma_start(offsets[:], offs)
+
+        xs_table = sb("xs_table", [P, T], U8)
+        nc.gpsimd.memset(xs_table[:].bitcast(I32), 0)
+        w2s_raw = sb("w2s_raw", [P, N], U8)
+        nc.gpsimd.memset(w2s_raw[:].bitcast(I32), 0)
+
+        w1_raw = [sb("w1_raw%d" % g, [P, PACK, H], F32) for g in range(PASSES)]
+        w1_rows = w1.rearrange("(g p j) c -> g p j c", g=PASSES, j=PACK)
+        w2w_raw = sb("w2w_raw", [P, 2 * N], U8)
+        nc.sync.dma_start(w2w_raw[:].bitcast(I32), w2_words[0].bitcast(I32))
+        nc.sync.dma_start(w1_raw[0][:], w1_rows[0])
+        for q in range(4):
+            nc.sync.dma_start(
+                xs_table[32 * q : 32 * q + 4 * PASSES, :].bitcast(I32),
+                x_scales[:, 4 * q : 4 * q + 4, :].bitcast(I32),
+            )
+        nc.sync.dma_start(w1_raw[1][:], w1_rows[1])
+        for q in range(4):
+            nc.sync.dma_start(
+                w2s_raw[32 * q : 32 * q + 4, :].bitcast(I32),
+                w2_scales[0, 4 * q : 4 * q + 4, :].bitcast(I32),
+            )
+        x_table = [sb("x_table%d" % g, [P, T], U32) for g in range(PASSES)]
+        for g in range(PASSES):
+            nc.sync.dma_start(
+                x_table[g][:].bitcast(I32), x_words[g].rearrange("p c r -> p (c r)").bitcast(I32)
+            )
+        mask_rows = mask.rearrange("(p t) c -> t p c", t=PACK)
+        out_rows = out_0.rearrange("(p t) c -> t p c", t=PACK)
+
+        w2_codes = sb("w2_codes", [P, 2 * N], U8)
+        nc.vector.tensor_copy(
+            w2_codes[:].rearrange("p (t m b) -> p m t b", t=PACK, b=2),
+            w2w_raw[:].rearrange("p (m t b) -> p m t b", t=PACK, b=2),
+        )
+        xs = sb("xs", [P, S], U8)
+        nc.vector.tensor_copy(xs[:], xs_table[:].indirect(offsets[:]))
+
+        w1_codes, w1_scales = [], []
+        for g in range(PASSES):
+            grouped = sb("w1_grouped%d" % g, [P, PACK * H], BF16)
+            dst = grouped[:].rearrange("p (t m j) -> p m j t", t=PACK, j=PACK)
+            src = w1_raw[g][:].rearrange("p j (m t) -> p m j t", t=PACK)
+            cut = SCALAR_SHARE[g]
+            nc.scalar.activation(dst[:, :cut], src[:, :cut], COPY)
+            nc.vector.tensor_copy(dst[:, cut:], src[:, cut:])
+            codes = sb("w1_codes%d" % g, [P, H], U32)
+            scales = sb("w1_scales%d" % g, [P, H], U8)
+            nc.vector.quantize_mx(out=codes[:].bitcast(FP8X4), scales=scales[:], in_=grouped[:])
+            w1_codes.append(codes)
+            w1_scales.append(scales)
+            if g == 0:
+                w2_scale = sb("w2_scale", [P, N], U8)
+                nc.vector.tensor_copy(
+                    w2_scale[:].rearrange("p (t m) -> p m t", t=PACK),
+                    w2s_raw[:].rearrange("p (m t) -> p m t", t=PACK),
+                )
+
+        spent = ("w1_raw0", "w1_grouped0", "w1_raw1", "w1_grouped1")
+        window = [sb("window%d" % t, [P, T], F32, tag=spent[t]) for t in range(PACK)]
+        for t in range(PACK):
+            nc.sync.dma_start(window[t][:], mask_rows[t])
+
+        xq = [sb("xq%d" % g, [P, S], U32) for g in range(PASSES)]
+        h_codes = sb("h_codes", [P, S], U32)
+        h_scales = sb("h_scales", [P, S], U8)
+        y = sb("y", [P, PACK, S], F32)
+
+        def cols(first, last):
+            return slice(first * CHUNK, last * CHUNK)
+
+        def entries(first, last):
+            return offsets[:, first * CHUNK // 16 : last * CHUNK // 16]
+
+        def gather(g, first, last):
+            nc.vector.tensor_copy(xq[g][:, cols(first, last)], x_table[g][:].indirect(entries(first, last)))
+
+        def first_layer(c):
+            acc = psum.tile([P, PACK, CHUNK], F32, name="acc", tag="bank%d" % c)
+            span = cols(c, c + 1)
+            for t in range(PACK):
+                for g in range(PASSES):
+                    nc.tensor.matmul_mx(
+                        out=acc[:, t, :],
+                        lhsT=w1_codes[g][:, t * P : (t + 1) * P].bitcast(FP8X4),
+                        lhsT_scale=w1_scales[g][:, t * P : (t + 1) * P],
+                        rhs=xq[g][:, span].bitcast(FP8X4),
+                        rhs_scale=xs[4 * g :, span],
+                        start=(g == 0),
+                        stop=(g == PASSES - 1),
+                    )
+            h = sb("h%d" % c, [P, CHUNK * PACK], BF16)
+            nc.scalar.activation(
+                h[:].rearrange("p (n t) -> p n t", t=PACK), acc[:].rearrange("p t n -> p n t"), RELU
+            )
+            nc.vector.quantize_mx(out=h_codes[:, span].bitcast(FP8X4), scales=h_scales[:, span], in_=h[:])
+
+        def second_layer(t0, t1, first, last, tag):
+            span = cols(first, last)
+            acc = psum.tile([P, t1 - t0, (last - first) * CHUNK], F32, name="acc", tag=tag)
+            for t in range(t0, t1):
+                nc.tensor.matmul_mx(
+                    out=acc[:, t - t0, :],
+                    lhsT=w2_codes[:, 2 * t * P : 2 * (t + 1) * P].bitcast(FP4X4),
+                    lhsT_scale=w2_scale[:, t * P : (t + 1) * P],
+                    rhs=h_codes[:, span].bitcast(FP8X4),
+                    rhs_scale=h_scales[:, span],
+                    start=True,
+                    stop=True,
+                )
+            nc.scalar.activation(y[:, t0:t1, span], acc[:], COPY)
+
+        def scatter(t, first, last):
+            nc.vector.tensor_copy(window[t][:].indirect(entries(first, last)), y[:, t, cols(first, last)])
+
+        for first, last in ((0, 1), (1, 2), (2, 4)):
+            for g in range(PASSES):
+                gather(g, first, last)
+        first_layer(0)
+        first_layer(1)
+        second_layer(0, 2, 0, 1, "bank4")
+        first_layer(2)
+        first_layer(3)
+        scatter(0, 0, 1)
+        scatter(1, 0, 1)
+        second_layer(0, 2, 1, 2, "bank5")
+        scatter(0, 1, 2)
+        scatter(1, 1, 2)
+        second_layer(0, 1, 2, 4, "bank6")
+        scatter(0, 2, 4)
+        second_layer(1, 2, 2, 4, "bank7")
+        scatter(1, 2, 4)
+        second_layer(2, 3, 0, 4, "bank0")
+        second_layer(3, 4, 0, 4, "bank1")
+
+        rounded = [sb("rounded%d" % u, [P, HALF, PACK], BF16) for u in range(2)]
+        out_codes = sb("out_codes", [P, T], U32)
+        out_scales = sb("out_scales", [P, T], U8)
+
+        def half(u):
+            return slice(u * HALF, (u + 1) * HALF)
+
+        for t in range(PACK):
+            if t > 1:
+                scatter(t, 0, CHUNKS)
+            nc.sync.dma_start(out_rows[t], window[t][:])
+            for u in range(2):
+                src = window[t][:, half(u)]
+                if t == PACK - 1:
+                    nc.vector.tensor_copy(rounded[u][:, :, t], src)
+                else:
+                    nc.scalar.activation(rounded[u][:, :, t], src, COPY)
+                if t == PACK - 2:
+                    nc.scalar.activation(
+                        rounded[u][:, HALF - 1, t:], src[:, HALF - 1 :].to_broadcast([P, 2]), COPY
+                    )
+
+        words_out = out_1[0].rearrange("p c r -> p (c r)").bitcast(I32)
+        for u in range(2):
+            nc.vector.quantize_mx(
+                out=out_codes[:, half(u)].bitcast(FP8X4),
+                scales=out_scales[:, half(u)],
+                in_=rounded[u][:].rearrange("p c t -> p (c t)"),
+            )
+            nc.sync.dma_start(words_out[:, half(u)], out_codes[:, half(u)].bitcast(I32))
+        for q in range(4):
+            queue = nc.scalar if q % 2 else nc.sync
+            queue.dma_start(
+                out_2[0, 4 * q : 4 * q + 4, :].bitcast(I32), out_scales[32 * q : 32 * q + 4, :].bitcast(I32)
+            )

@@ -42,7 +42,12 @@ def tile_picked_zmae_mlprelu_po_kernel(
         xs_table = sb("xs_table", [P, T], U8)
         nc.gpsimd.memset(xs_table[:].bitcast(I32), 0)
         w2s_raw = sb("w2s_raw", [P, N], U8)
-        nc.gpsimd.memset(w2s_raw[:].bitcast(I32), 0)
+        for q in range(4):
+            rows = w2_scales[0, 4 * q : 4 * q + 4, :].bitcast(I32)
+            nc.scalar.dma_start(
+                w2s_raw[32 * q : 32 * (q + 1), :].bitcast(I32),
+                rows.unsqueeze(0).to_broadcast([8, 4, N // 4]),
+            )
 
         w1_raw = [sb("w1_raw%d" % g, [P, PACK, H], F32) for g in range(PASSES)]
         w1_rows = w1.rearrange("(g p j) c -> g p j c", g=PASSES, j=PACK)
@@ -55,11 +60,6 @@ def tile_picked_zmae_mlprelu_po_kernel(
                 x_scales[:, 4 * q : 4 * q + 4, :].bitcast(I32),
             )
         nc.sync.dma_start(w1_raw[1][:], w1_rows[1])
-        for q in range(4):
-            nc.sync.dma_start(
-                w2s_raw[32 * q : 32 * q + 4, :].bitcast(I32),
-                w2_scales[0, 4 * q : 4 * q + 4, :].bitcast(I32),
-            )
         x_table = [sb("x_table%d" % g, [P, T], U32) for g in range(PASSES)]
         for g in range(PASSES):
             nc.sync.dma_start(
@@ -72,6 +72,11 @@ def tile_picked_zmae_mlprelu_po_kernel(
         nc.vector.tensor_copy(
             w2_codes[:].rearrange("p (t m b) -> p m t b", t=PACK, b=2),
             w2w_raw[:].rearrange("p (m t b) -> p m t b", t=PACK, b=2),
+        )
+        w2_scale = sb("w2_scale", [P, N], U8)
+        nc.vector.tensor_copy(
+            w2_scale[:].rearrange("p (t m) -> p m t", t=PACK),
+            w2s_raw[:].rearrange("p (m t) -> p m t", t=PACK),
         )
         xs = sb("xs", [P, S], U8)
         nc.vector.tensor_copy(xs[:], xs_table[:].indirect(offsets[:]))
@@ -89,12 +94,6 @@ def tile_picked_zmae_mlprelu_po_kernel(
             nc.vector.quantize_mx(out=codes[:].bitcast(FP8X4), scales=scales[:], in_=grouped[:])
             w1_codes.append(codes)
             w1_scales.append(scales)
-            if g == 0:
-                w2_scale = sb("w2_scale", [P, N], U8)
-                nc.vector.tensor_copy(
-                    w2_scale[:].rearrange("p (t m) -> p m t", t=PACK),
-                    w2s_raw[:].rearrange("p (m t) -> p m t", t=PACK),
-                )
 
         spent = ("w1_raw0", "w1_grouped0", "w1_raw1", "w1_grouped1")
         window = [sb("window%d" % t, [P, T], F32, tag=spent[t]) for t in range(PACK)]
@@ -130,12 +129,11 @@ def tile_picked_zmae_mlprelu_po_kernel(
                         stop=(g == PASSES - 1),
                     )
             h = sb("h%d" % c, [P, CHUNK * PACK], BF16)
-            nc.scalar.activation(
-                h[:].rearrange("p (n t) -> p n t", t=PACK), acc[:].rearrange("p t n -> p n t"), RELU
-            )
+            dst, src = h[:].rearrange("p (n t) -> p n t", t=PACK), acc[:].rearrange("p t n -> p n t")
+            nc.scalar.activation(dst, src, RELU)
             nc.vector.quantize_mx(out=h_codes[:, span].bitcast(FP8X4), scales=h_scales[:, span], in_=h[:])
 
-        def second_layer(t0, t1, first, last, tag):
+        def second_layer(t0, t1, first, last, tag, on_vector=False):
             span = cols(first, last)
             acc = psum.tile([P, t1 - t0, (last - first) * CHUNK], F32, name="acc", tag=tag)
             for t in range(t0, t1):
@@ -148,7 +146,10 @@ def tile_picked_zmae_mlprelu_po_kernel(
                     start=True,
                     stop=True,
                 )
-            nc.scalar.activation(y[:, t0:t1, span], acc[:], COPY)
+            if on_vector:
+                nc.vector.tensor_copy(y[:, t0:t1, span], acc[:])
+            else:
+                nc.scalar.activation(y[:, t0:t1, span], acc[:], COPY)
 
         def scatter(t, first, last):
             nc.vector.tensor_copy(window[t][:].indirect(entries(first, last)), y[:, t, cols(first, last)])
@@ -158,51 +159,54 @@ def tile_picked_zmae_mlprelu_po_kernel(
                 gather(g, first, last)
         first_layer(0)
         first_layer(1)
-        second_layer(0, 2, 0, 1, "bank4")
+        second_layer(0, 1, 0, 1, "bank4", on_vector=True)
+        second_layer(1, 2, 0, 1, "bank5")
         first_layer(2)
         first_layer(3)
         scatter(0, 0, 1)
         scatter(1, 0, 1)
-        second_layer(0, 2, 1, 2, "bank5")
+        second_layer(0, 2, 1, 2, "bank6")
         scatter(0, 1, 2)
         scatter(1, 1, 2)
-        second_layer(0, 1, 2, 4, "bank6")
+        second_layer(0, 1, 2, 4, "bank7")
         scatter(0, 2, 4)
-        second_layer(1, 2, 2, 4, "bank7")
+        second_layer(1, 2, 2, 4, "bank0")
         scatter(1, 2, 4)
-        second_layer(2, 3, 0, 4, "bank0")
-        second_layer(3, 4, 0, 4, "bank1")
+        second_layer(2, 3, 0, 4, "bank1")
+        second_layer(3, 4, 0, 4, "bank2")
 
-        rounded = [sb("rounded%d" % u, [P, HALF, PACK], BF16) for u in range(2)]
+        pairs = sb("pairs", [P, 2, T, 2], BF16)
+        rounded = sb("rounded", [P, T, 2], I32)
         out_codes = sb("out_codes", [P, T], U32)
         out_scales = sb("out_scales", [P, T], U8)
-
-        def half(u):
-            return slice(u * HALF, (u + 1) * HALF)
+        halves = (slice(0, HALF), slice(HALF, T))
+        seam = slice(HALF - 1, HALF + 1)
+        last = PACK - 1
 
         for t in range(PACK):
             if t > 1:
                 scatter(t, 0, CHUNKS)
             nc.sync.dma_start(out_rows[t], window[t][:])
-            for u in range(2):
-                src = window[t][:, half(u)]
-                if t == PACK - 1:
-                    nc.vector.tensor_copy(rounded[u][:, :, t], src)
-                else:
-                    nc.scalar.activation(rounded[u][:, :, t], src, COPY)
-                if t == PACK - 2:
-                    nc.scalar.activation(
-                        rounded[u][:, HALF - 1, t:], src[:, HALF - 1 :].to_broadcast([P, 2]), COPY
-                    )
+            if t < last:
+                nc.scalar.activation(pairs[:, t // 2, :, t % 2], window[t][:], COPY)
+            if t == last - 1:
+                nc.scalar.activation(
+                    pairs[:, 1, seam, :], window[t][:, seam].unsqueeze(2).to_broadcast([P, 2, 2]), COPY
+                )
+        nc.vector.tensor_copy(pairs[:, 1, halves[0], 1], window[last][:, halves[0]])
+        nc.scalar.activation(pairs[:, 1, halves[1], 1], window[last][:, halves[1]], COPY)
 
+        pair_words = pairs[:].rearrange("p u c e -> p u (c e)").bitcast(I32).rearrange("p u c -> p c u")
         words_out = out_1[0].rearrange("p c r -> p (c r)").bitcast(I32)
-        for u in range(2):
+        for span in halves:
+            nc.vector.tensor_copy(rounded[:, span, :], pair_words[:, span, :])
+        for span in halves:
             nc.vector.quantize_mx(
-                out=out_codes[:, half(u)].bitcast(FP8X4),
-                scales=out_scales[:, half(u)],
-                in_=rounded[u][:].rearrange("p c t -> p (c t)"),
+                out=out_codes[:, span].bitcast(FP8X4),
+                scales=out_scales[:, span],
+                in_=rounded[:, span, :].rearrange("p c u -> p (c u)").bitcast(BF16),
             )
-            nc.sync.dma_start(words_out[:, half(u)], out_codes[:, half(u)].bitcast(I32))
+            nc.sync.dma_start(words_out[:, span], out_codes[:, span].bitcast(I32))
         for q in range(4):
             queue = nc.scalar if q % 2 else nc.sync
             queue.dma_start(

@@ -22,7 +22,7 @@ PASSES = K // (P * PACK)
 CHUNK = 128
 CHUNKS = S // CHUNK
 HALF = T // 2
-SCALAR_SHARE = (96, 48)
+SCALAR_SHARE = (96, 54)
 
 
 def tile_picked_zmae_mlprelu_po_kernel(
@@ -81,6 +81,17 @@ def tile_picked_zmae_mlprelu_po_kernel(
         xs = sb("xs", [P, S], U8)
         nc.vector.tensor_copy(xs[:], xs_table[:].indirect(offsets[:]))
 
+        xq = [sb("xq%d" % g, [P, S], U32) for g in range(PASSES)]
+
+        def cols(first, last):
+            return slice(first * CHUNK, last * CHUNK)
+
+        def entries(first, last):
+            return offsets[:, first * CHUNK // 16 : last * CHUNK // 16]
+
+        def gather(g, first, last):
+            nc.vector.tensor_copy(xq[g][:, cols(first, last)], x_table[g][:].indirect(entries(first, last)))
+
         w1_codes, w1_scales = [], []
         for g in range(PASSES):
             grouped = sb("w1_grouped%d" % g, [P, PACK * H], BF16)
@@ -89,6 +100,8 @@ def tile_picked_zmae_mlprelu_po_kernel(
             cut = SCALAR_SHARE[g]
             nc.scalar.activation(dst[:, :cut], src[:, :cut], COPY)
             nc.vector.tensor_copy(dst[:, cut:], src[:, cut:])
+            if g == PASSES - 1:
+                gather(0, 0, 1)
             codes = sb("w1_codes%d" % g, [P, H], U32)
             scales = sb("w1_scales%d" % g, [P, H], U8)
             nc.vector.quantize_mx(out=codes[:].bitcast(FP8X4), scales=scales[:], in_=grouped[:])
@@ -100,19 +113,10 @@ def tile_picked_zmae_mlprelu_po_kernel(
         for t in range(PACK):
             nc.sync.dma_start(window[t][:], mask_rows[t])
 
-        xq = [sb("xq%d" % g, [P, S], U32) for g in range(PASSES)]
+        h = sb("h", [P, S, PACK], BF16)
         h_codes = sb("h_codes", [P, S], U32)
         h_scales = sb("h_scales", [P, S], U8)
         y = sb("y", [P, PACK, S], F32)
-
-        def cols(first, last):
-            return slice(first * CHUNK, last * CHUNK)
-
-        def entries(first, last):
-            return offsets[:, first * CHUNK // 16 : last * CHUNK // 16]
-
-        def gather(g, first, last):
-            nc.vector.tensor_copy(xq[g][:, cols(first, last)], x_table[g][:].indirect(entries(first, last)))
 
         def first_layer(c):
             acc = psum.tile([P, PACK, CHUNK], F32, name="acc", tag="bank%d" % c)
@@ -128,10 +132,15 @@ def tile_picked_zmae_mlprelu_po_kernel(
                         start=(g == 0),
                         stop=(g == PASSES - 1),
                     )
-            h = sb("h%d" % c, [P, CHUNK * PACK], BF16)
-            dst, src = h[:].rearrange("p (n t) -> p n t", t=PACK), acc[:].rearrange("p t n -> p n t")
-            nc.scalar.activation(dst, src, RELU)
-            nc.vector.quantize_mx(out=h_codes[:, span].bitcast(FP8X4), scales=h_scales[:, span], in_=h[:])
+            nc.scalar.activation(h[:, span, :], acc[:].rearrange("p t n -> p n t"), RELU)
+
+        def quantise_h(first, last):
+            span = cols(first, last)
+            nc.vector.quantize_mx(
+                out=h_codes[:, span].bitcast(FP8X4),
+                scales=h_scales[:, span],
+                in_=h[:, span, :].rearrange("p n t -> p (n t)"),
+            )
 
         def second_layer(t0, t1, first, last, tag, on_vector=False):
             span = cols(first, last)
@@ -154,15 +163,20 @@ def tile_picked_zmae_mlprelu_po_kernel(
         def scatter(t, first, last):
             nc.vector.tensor_copy(window[t][:].indirect(entries(first, last)), y[:, t, cols(first, last)])
 
-        for first, last in ((0, 1), (1, 2), (2, 4)):
+        gather(1, 0, 1)
+        for first, last in ((1, 2), (2, 4)):
             for g in range(PASSES):
                 gather(g, first, last)
         first_layer(0)
+        quantise_h(0, 1)
         first_layer(1)
+        quantise_h(1, 2)
         second_layer(0, 1, 0, 1, "bank4", on_vector=True)
         second_layer(1, 2, 0, 1, "bank5")
         first_layer(2)
+        quantise_h(2, 3)
         first_layer(3)
+        quantise_h(3, 4)
         scatter(0, 0, 1)
         scatter(1, 0, 1)
         second_layer(0, 2, 1, 2, "bank6")
@@ -175,36 +189,43 @@ def tile_picked_zmae_mlprelu_po_kernel(
         second_layer(2, 3, 0, 4, "bank1")
         second_layer(3, 4, 0, 4, "bank2")
 
-        pairs = sb("pairs", [P, 2, T, 2], BF16)
-        rounded = sb("rounded", [P, T, 2], I32)
+        quarter = T // 4
+        spans = (slice(0, quarter), slice(quarter, HALF), slice(HALF, T))
+        pairs = [sb("pairs%d" % u, [P, 2, quarter, 2], BF16) for u in range(2)]
+        rounded = [sb("rounded%d" % u, [P, span.stop - span.start, PACK], BF16) for u, span in enumerate(spans)]
         out_codes = sb("out_codes", [P, T], U32)
         out_scales = sb("out_scales", [P, T], U8)
-        halves = (slice(0, HALF), slice(HALF, T))
-        seam = slice(HALF - 1, HALF + 1)
         last = PACK - 1
 
         for t in range(PACK):
             if t > 1:
                 scatter(t, 0, CHUNKS)
             nc.sync.dma_start(out_rows[t], window[t][:])
-            if t < last:
-                nc.scalar.activation(pairs[:, t // 2, :, t % 2], window[t][:], COPY)
+            for u in range(2):
+                src = window[t][:, spans[u]]
+                if t < last:
+                    nc.scalar.activation(pairs[u][:, t // 2, :, t % 2], src, COPY)
+                else:
+                    nc.vector.tensor_copy(pairs[u][:, t // 2, :, t % 2], src)
             if t == last - 1:
-                nc.scalar.activation(
-                    pairs[:, 1, seam, :], window[t][:, seam].unsqueeze(2).to_broadcast([P, 2, 2]), COPY
-                )
-        nc.vector.tensor_copy(pairs[:, 1, halves[0], 1], window[last][:, halves[0]])
-        nc.scalar.activation(pairs[:, 1, halves[1], 1], window[last][:, halves[1]], COPY)
+                for u in range(2):
+                    first = spans[u].start
+                    nc.scalar.activation(
+                        pairs[u][:, 1, 0, :], window[t][:, first : first + 1].to_broadcast([P, 2]), COPY
+                    )
+            nc.scalar.activation(rounded[2][:, :, t], window[t][:, spans[2]], COPY)
 
-        pair_words = pairs[:].rearrange("p u c e -> p u (c e)").bitcast(I32).rearrange("p u c -> p c u")
+        for u in range(2):
+            nc.vector.tensor_copy(
+                rounded[u][:].bitcast(I32),
+                pairs[u][:].rearrange("p u c e -> p u (c e)").bitcast(I32).rearrange("p u c -> p c u"),
+            )
         words_out = out_1[0].rearrange("p c r -> p (c r)").bitcast(I32)
-        for span in halves:
-            nc.vector.tensor_copy(rounded[:, span, :], pair_words[:, span, :])
-        for span in halves:
+        for u, span in enumerate(spans):
             nc.vector.quantize_mx(
                 out=out_codes[:, span].bitcast(FP8X4),
                 scales=out_scales[:, span],
-                in_=rounded[:, span, :].rearrange("p c u -> p (c u)").bitcast(BF16),
+                in_=rounded[u][:].rearrange("p c t -> p (c t)"),
             )
             nc.sync.dma_start(words_out[:, span], out_codes[:, span].bitcast(I32))
         for q in range(4):

@@ -22,7 +22,9 @@ PASSES = K // (P * PACK)
 CHUNK = 128
 CHUNKS = S // CHUNK
 HALF = T // 2
-SCALAR_SHARE = (96, 54)
+SCALAR_SHARE = (64, 40)
+WARM_PASSES = 3
+PAIRED = 448
 
 
 def tile_picked_zmae_mlprelu_po_kernel(
@@ -40,48 +42,39 @@ def tile_picked_zmae_mlprelu_po_kernel(
         nc.sync.dma_start(offsets[:], offs)
 
         xs_table = sb("xs_table", [P, T], U8)
-        nc.gpsimd.memset(xs_table[:].bitcast(I32), 0)
+        nc.vector.memset(xs_table[:].bitcast(I32), 0)
         w2s_raw = sb("w2s_raw", [P, N], U8)
+        nc.gpsimd.memset(w2s_raw[:].bitcast(I32), 0)
         for q in range(4):
-            rows = w2_scales[0, 4 * q : 4 * q + 4, :].bitcast(I32)
-            nc.scalar.dma_start(
-                w2s_raw[32 * q : 32 * (q + 1), :].bitcast(I32),
-                rows.unsqueeze(0).to_broadcast([8, 4, N // 4]),
+            nc.gpsimd.dma_start(
+                w2s_raw[32 * q : 32 * q + 4, :].bitcast(I32), w2_scales[0, 4 * q : 4 * q + 4, :].bitcast(I32)
             )
-
-        w1_raw = [sb("w1_raw%d" % g, [P, PACK, H], F32) for g in range(PASSES)]
-        w1_rows = w1.rearrange("(g p j) c -> g p j c", g=PASSES, j=PACK)
         w2w_raw = sb("w2w_raw", [P, 2 * N], U8)
         nc.sync.dma_start(w2w_raw[:].bitcast(I32), w2_words[0].bitcast(I32))
-        nc.sync.dma_start(w1_raw[0][:], w1_rows[0])
+
+        w1_rows = w1.rearrange("(g p j) c -> g p j c", g=PASSES, j=PACK)
+        w1_raw = [sb("w1_raw%d" % g, [P, PACK, H], F32) for g in range(PASSES)]
+        x_table = [sb("x_table%d" % g, [P, T], U32) for g in range(PASSES)]
+
+        def load_w1(g):
+            nc.sync.dma_start(w1_raw[g][:], w1_rows[g])
+
+        def load_x(g):
+            nc.sync.dma_start(
+                x_table[g][:].bitcast(I32), x_words[g].rearrange("p c r -> p (c r)").bitcast(I32)
+            )
+
+        load_x(0)
         for q in range(4):
             nc.sync.dma_start(
                 xs_table[32 * q : 32 * q + 4 * PASSES, :].bitcast(I32),
                 x_scales[:, 4 * q : 4 * q + 4, :].bitcast(I32),
             )
-        nc.sync.dma_start(w1_raw[1][:], w1_rows[1])
-        x_table = [sb("x_table%d" % g, [P, T], U32) for g in range(PASSES)]
-        for g in range(PASSES):
-            nc.sync.dma_start(
-                x_table[g][:].bitcast(I32), x_words[g].rearrange("p c r -> p (c r)").bitcast(I32)
-            )
+        load_w1(0)
+        load_w1(1)
+        load_x(1)
         mask_rows = mask.rearrange("(p t) c -> t p c", t=PACK)
         out_rows = out_0.rearrange("(p t) c -> t p c", t=PACK)
-
-        w2_codes = sb("w2_codes", [P, 2 * N], U8)
-        nc.vector.tensor_copy(
-            w2_codes[:].rearrange("p (t m b) -> p m t b", t=PACK, b=2),
-            w2w_raw[:].rearrange("p (m t b) -> p m t b", t=PACK, b=2),
-        )
-        w2_scale = sb("w2_scale", [P, N], U8)
-        nc.vector.tensor_copy(
-            w2_scale[:].rearrange("p (t m) -> p m t", t=PACK),
-            w2s_raw[:].rearrange("p (m t) -> p m t", t=PACK),
-        )
-        xs = sb("xs", [P, S], U8)
-        nc.vector.tensor_copy(xs[:], xs_table[:].indirect(offsets[:]))
-
-        xq = [sb("xq%d" % g, [P, S], U32) for g in range(PASSES)]
 
         def cols(first, last):
             return slice(first * CHUNK, last * CHUNK)
@@ -89,137 +82,184 @@ def tile_picked_zmae_mlprelu_po_kernel(
         def entries(first, last):
             return offsets[:, first * CHUNK // 16 : last * CHUNK // 16]
 
-        def gather(g, first, last):
-            nc.vector.tensor_copy(xq[g][:, cols(first, last)], x_table[g][:].indirect(entries(first, last)))
+        w1_codes = [sb("w1_codes%d" % g, [P, H], U32) for g in range(PASSES)]
+        w1_scales = [sb("w1_scales%d" % g, [P, H], U8) for g in range(PASSES)]
 
-        w1_codes, w1_scales = [], []
-        for g in range(PASSES):
-            grouped = sb("w1_grouped%d" % g, [P, PACK * H], BF16)
+        def round_w1(g):
+            grouped = sb("w1_grouped%d" % g, [P, PACK * H], BF16, tag="w1_grouped")
             dst = grouped[:].rearrange("p (t m j) -> p m j t", t=PACK, j=PACK)
             src = w1_raw[g][:].rearrange("p j (m t) -> p m j t", t=PACK)
             cut = SCALAR_SHARE[g]
             nc.scalar.activation(dst[:, :cut], src[:, :cut], COPY)
             nc.vector.tensor_copy(dst[:, cut:], src[:, cut:])
-            if g == PASSES - 1:
-                gather(0, 0, 1)
-            codes = sb("w1_codes%d" % g, [P, H], U32)
-            scales = sb("w1_scales%d" % g, [P, H], U8)
-            nc.vector.quantize_mx(out=codes[:].bitcast(FP8X4), scales=scales[:], in_=grouped[:])
-            w1_codes.append(codes)
-            w1_scales.append(scales)
+            return grouped
 
-        spent = ("w1_raw0", "w1_grouped0", "w1_raw1", "w1_grouped1")
-        window = [sb("window%d" % t, [P, T], F32, tag=spent[t]) for t in range(PACK)]
-        for t in range(PACK):
+        def quantise_w1(g, t0, t1, grouped):
+            nc.vector.quantize_mx(
+                out=w1_codes[g][:, t0 * P : t1 * P].bitcast(FP8X4),
+                scales=w1_scales[g][:, t0 * P : t1 * P],
+                in_=grouped[:, t0 * PACK * P : t1 * PACK * P],
+            )
+
+        def gather_x1(dst, first, last):
+            nc.vector.tensor_copy(dst, x_table[1][:].indirect(entries(first, last)))
+
+        w2_codes = sb("w2_codes", [P, 2 * N], U8)
+        nc.vector.tensor_copy(
+            w2_codes[:].rearrange("p (t m b) -> p m t b", t=PACK, b=2),
+            w2w_raw[:].rearrange("p (m t b) -> p m t b", t=PACK, b=2),
+        )
+        xs = sb("xs", [P, S], U8)
+        xq0 = sb("xq0", [P, S], U32)
+        nc.vector.tensor_copy(xq0[:], x_table[0][:].indirect(offsets[:]))
+        nc.vector.tensor_copy(xs[:], xs_table[:].indirect(offsets[:]))
+        quantise_w1(0, 0, PACK, round_w1(0))
+        warm = psum.tile([P, S], F32, name="warm", tag="bank5")
+        for t in range(WARM_PASSES):
+            nc.tensor.matmul_mx(
+                out=warm[:],
+                lhsT=w1_codes[0][:, t * P : (t + 1) * P].bitcast(FP8X4),
+                lhsT_scale=w1_scales[0][:, t * P : (t + 1) * P],
+                rhs=xq0[:].bitcast(FP8X4),
+                rhs_scale=xs[:],
+                start=True,
+                stop=True,
+            )
+        grouped = round_w1(1)
+        xq1 = [sb("xq1_early", [P, S // 2], U32, tag="w1_raw1")]
+        quantise_w1(1, 0, 1, grouped)
+        gather_x1(xq1[0][:, cols(0, 1)], 0, 1)
+        quantise_w1(1, 1, 2, grouped)
+        quantise_w1(1, 2, 4, grouped)
+        gather_x1(xq1[0][:, cols(1, 2)], 1, 2)
+
+        window = []
+
+        def load_window(t, tag):
+            window.append(sb("window%d" % t, [P, T], F32, tag=tag))
             nc.sync.dma_start(window[t][:], mask_rows[t])
 
-        h = sb("h", [P, S, PACK], BF16)
-        h_codes = sb("h_codes", [P, S], U32)
-        h_scales = sb("h_scales", [P, S], U8)
-        y = sb("y", [P, PACK, S], F32)
+        load_window(0, "w2w_raw")
+        load_window(1, "w1_raw0")
 
-        def first_layer(c):
-            acc = psum.tile([P, PACK, CHUNK], F32, name="acc", tag="bank%d" % c)
+        parts = ((0, 1), (1, 2), (2, 4))
+        h = [sb("h%d" % u, [P, (last - first) * CHUNK, PACK], BF16) for u, (first, last) in enumerate(parts)]
+        h_codes = [sb("h_codes%d" % u, [P, (last - first) * CHUNK], U32) for u, (first, last) in enumerate(parts)]
+        h_scales = []
+
+        def first_layer(c, t0, t1, tag, on_vector=False):
+            acc = psum.tile([P, t1 - t0, CHUNK], F32, name="acc", tag=tag)
             span = cols(c, c + 1)
-            for t in range(PACK):
+            moving = (xq0[:, span], xq1[c // 2][:, cols(c % 2, c % 2 + 1)])
+            for t in range(t0, t1):
                 for g in range(PASSES):
                     nc.tensor.matmul_mx(
-                        out=acc[:, t, :],
+                        out=acc[:, t - t0, :],
                         lhsT=w1_codes[g][:, t * P : (t + 1) * P].bitcast(FP8X4),
                         lhsT_scale=w1_scales[g][:, t * P : (t + 1) * P],
-                        rhs=xq[g][:, span].bitcast(FP8X4),
+                        rhs=moving[g].bitcast(FP8X4),
                         rhs_scale=xs[4 * g :, span],
                         start=(g == 0),
                         stop=(g == PASSES - 1),
                     )
-            nc.scalar.activation(h[:, span, :], acc[:].rearrange("p t n -> p n t"), RELU)
+            dst = h[c][:] if c < 2 else h[2][:, cols(c - 2, c - 1), :]
+            src = acc[:].rearrange("p t n -> p n t")
+            if on_vector:
+                nc.vector.tensor_scalar_max(dst[:, :, t0:t1], src, 0.0)
+            else:
+                nc.scalar.activation(dst[:, :, t0:t1], src, RELU)
 
-        def quantise_h(first, last):
-            span = cols(first, last)
+        def quantise_h(u, tag=""):
+            h_scales.append(sb("h_scales%d" % u, [P, (parts[u][1] - parts[u][0]) * CHUNK], U8, tag=tag))
             nc.vector.quantize_mx(
-                out=h_codes[:, span].bitcast(FP8X4),
-                scales=h_scales[:, span],
-                in_=h[:, span, :].rearrange("p n t -> p (n t)"),
+                out=h_codes[u][:].bitcast(FP8X4),
+                scales=h_scales[u][:],
+                in_=h[u][:].rearrange("p n t -> p (n t)"),
             )
 
-        def second_layer(t0, t1, first, last, tag, on_vector=False):
-            span = cols(first, last)
-            acc = psum.tile([P, t1 - t0, (last - first) * CHUNK], F32, name="acc", tag=tag)
+        def second_layer(t0, t1, u0, u1, tag, on_vector=False):
+            first, last = parts[u0][0], parts[u1 - 1][1]
+            width = (last - first) * CHUNK
+            acc = psum.tile([P, t1 - t0, width], F32, name="acc", tag=tag)
             for t in range(t0, t1):
-                nc.tensor.matmul_mx(
-                    out=acc[:, t - t0, :],
-                    lhsT=w2_codes[:, 2 * t * P : 2 * (t + 1) * P].bitcast(FP4X4),
-                    lhsT_scale=w2_scale[:, t * P : (t + 1) * P],
-                    rhs=h_codes[:, span].bitcast(FP8X4),
-                    rhs_scale=h_scales[:, span],
-                    start=True,
-                    stop=True,
-                )
+                for u in range(u0, u1):
+                    nc.tensor.matmul_mx(
+                        out=acc[:, t - t0, cols(parts[u][0] - first, parts[u][1] - first)],
+                        lhsT=w2_codes[:, 2 * t * P : 2 * (t + 1) * P].bitcast(FP4X4),
+                        lhsT_scale=w2_scale[:, t * P : (t + 1) * P],
+                        rhs=h_codes[u][:].bitcast(FP8X4),
+                        rhs_scale=h_scales[u][:],
+                        start=True,
+                        stop=True,
+                    )
+            y = sb("y%d_%d" % (t0, u0), [P, t1 - t0, width], F32)
             if on_vector:
-                nc.vector.tensor_copy(y[:, t0:t1, span], acc[:])
+                nc.vector.tensor_copy(y[:], acc[:])
             else:
-                nc.scalar.activation(y[:, t0:t1, span], acc[:], COPY)
+                nc.scalar.activation(y[:], acc[:], COPY)
+            return y
 
-        def scatter(t, first, last):
-            nc.vector.tensor_copy(window[t][:].indirect(entries(first, last)), y[:, t, cols(first, last)])
+        def scatter(t, first, last, values):
+            nc.vector.tensor_copy(window[t][:].indirect(entries(first, last)), values)
 
-        gather(1, 0, 1)
-        for first, last in ((1, 2), (2, 4)):
-            for g in range(PASSES):
-                gather(g, first, last)
-        first_layer(0)
-        quantise_h(0, 1)
-        first_layer(1)
-        quantise_h(1, 2)
-        second_layer(0, 1, 0, 1, "bank4", on_vector=True)
-        second_layer(1, 2, 0, 1, "bank5")
-        first_layer(2)
-        quantise_h(2, 3)
-        first_layer(3)
-        quantise_h(3, 4)
-        scatter(0, 0, 1)
-        scatter(1, 0, 1)
-        second_layer(0, 2, 1, 2, "bank6")
-        scatter(0, 1, 2)
-        scatter(1, 1, 2)
-        second_layer(0, 1, 2, 4, "bank7")
-        scatter(0, 2, 4)
-        second_layer(1, 2, 2, 4, "bank0")
-        scatter(1, 2, 4)
-        second_layer(2, 3, 0, 4, "bank1")
-        second_layer(3, 4, 0, 4, "bank2")
+        w2_scale = sb("w2_scale", [P, N], U8, tag="w1_grouped")
+        nc.vector.tensor_copy(
+            w2_scale[:].rearrange("p (t m) -> p m t", t=PACK),
+            w2s_raw[:].rearrange("p (m t) -> p m t", t=PACK),
+        )
+        load_window(2, "w2s_raw")
+        first_layer(0, 0, 2, "bank0")
+        first_layer(0, 2, 4, "bank1")
+        quantise_h(0)
+        xq1.append(sb("xq1_late", [P, S // 2], U32, tag="h0"))
+        gather_x1(xq1[1][:], 2, 4)
+        y00 = second_layer(0, 1, 0, 1, "bank3")
+        y10 = second_layer(1, 2, 0, 1, "bank4")
+        first_layer(1, 0, 4, "bank2")
+        quantise_h(1)
+        scatter(0, 0, 1, y00[:, 0, :])
+        scatter(1, 0, 1, y10[:, 0, :])
+        first_layer(2, 0, 4, "bank0")
+        load_window(3, "h1")
+        y01 = second_layer(0, 2, 1, 2, "bank0")
+        first_layer(3, 0, 4, "bank1")
+        scatter(0, 1, 2, y01[:, 0, :])
+        quantise_h(2, tag="y1_0")
+        scatter(1, 1, 2, y01[:, 1, :])
+        y02 = second_layer(0, 1, 2, 3, "bank6")
+        scatter(0, 2, 4, y02[:, 0, :])
+        y12 = second_layer(1, 2, 2, 3, "bank7")
+        scatter(1, 2, 4, y12[:, 0, :])
+        y_late = {t: second_layer(t, t + 1, 0, 3, "bank%d" % t) for t in (2, 3)}
 
-        quarter = T // 4
-        spans = (slice(0, quarter), slice(quarter, HALF), slice(HALF, T))
-        pairs = [sb("pairs%d" % u, [P, 2, quarter, 2], BF16) for u in range(2)]
-        rounded = [sb("rounded%d" % u, [P, span.stop - span.start, PACK], BF16) for u, span in enumerate(spans)]
+        pairs = sb("pairs", [P, 2, PAIRED, 2], BF16)
         out_codes = sb("out_codes", [P, T], U32)
         out_scales = sb("out_scales", [P, T], U8)
         last = PACK - 1
+        spans = (slice(0, HALF), slice(HALF, HALF + T // 4), slice(HALF + T // 4, T))
+        rounded = [sb("rounded%d" % u, [P, span.stop - span.start, PACK], BF16) for u, span in enumerate(spans)]
+
+        def round_direct(t):
+            nc.scalar.activation(rounded[0][:, PAIRED:, t], window[t][:, PAIRED:HALF], COPY)
+            for u in (1, 2):
+                nc.scalar.activation(rounded[u][:, :, t], window[t][:, spans[u]], COPY)
 
         for t in range(PACK):
             if t > 1:
-                scatter(t, 0, CHUNKS)
+                scatter(t, 0, CHUNKS, y_late[t][:, 0, :])
             nc.sync.dma_start(out_rows[t], window[t][:])
-            for u in range(2):
-                src = window[t][:, spans[u]]
-                if t < last:
-                    nc.scalar.activation(pairs[u][:, t // 2, :, t % 2], src, COPY)
-                else:
-                    nc.vector.tensor_copy(pairs[u][:, t // 2, :, t % 2], src)
-            if t == last - 1:
-                for u in range(2):
-                    first = spans[u].start
-                    nc.scalar.activation(
-                        pairs[u][:, 1, 0, :], window[t][:, first : first + 1].to_broadcast([P, 2]), COPY
-                    )
-            nc.scalar.activation(rounded[2][:, :, t], window[t][:, spans[2]], COPY)
+            if t < last:
+                nc.scalar.activation(pairs[:, t // 2, :, t % 2], window[t][:, :PAIRED], COPY)
+                if t == last - 1:
+                    nc.scalar.activation(pairs[:, 1, 0, :], window[t][:, 0:1].to_broadcast([P, 2]), COPY)
+            else:
+                nc.vector.tensor_copy(pairs[:, t // 2, :, t % 2], window[t][:, :PAIRED])
+            round_direct(t)
 
-        for u in range(2):
-            nc.vector.tensor_copy(
-                rounded[u][:].bitcast(I32),
-                pairs[u][:].rearrange("p u c e -> p u (c e)").bitcast(I32).rearrange("p u c -> p c u"),
-            )
+        nc.vector.tensor_copy(
+            rounded[0][:, :PAIRED, :].bitcast(I32),
+            pairs[:].rearrange("p u c e -> p u (c e)").bitcast(I32).rearrange("p u c -> p c u"),
+        )
         words_out = out_1[0].rearrange("p c r -> p (c r)").bitcast(I32)
         for u, span in enumerate(spans):
             nc.vector.quantize_mx(

@@ -23,7 +23,6 @@ CHUNK = 128
 CHUNKS = S // CHUNK
 HALF = T // 2
 SCALAR_SHARE = (64, 40)
-WARM_PASSES = 3
 PAIRED = 448
 
 
@@ -114,17 +113,6 @@ def tile_picked_zmae_mlprelu_po_kernel(
         nc.vector.tensor_copy(xq0[:], x_table[0][:].indirect(offsets[:]))
         nc.vector.tensor_copy(xs[:], xs_table[:].indirect(offsets[:]))
         quantise_w1(0, 0, PACK, round_w1(0))
-        warm = psum.tile([P, S], F32, name="warm", tag="bank5")
-        for t in range(WARM_PASSES):
-            nc.tensor.matmul_mx(
-                out=warm[:],
-                lhsT=w1_codes[0][:, t * P : (t + 1) * P].bitcast(FP8X4),
-                lhsT_scale=w1_scales[0][:, t * P : (t + 1) * P],
-                rhs=xq0[:].bitcast(FP8X4),
-                rhs_scale=xs[:],
-                start=True,
-                stop=True,
-            )
         grouped = round_w1(1)
         xq1 = [sb("xq1_early", [P, S // 2], U32, tag="w1_raw1")]
         quantise_w1(1, 0, 1, grouped)

@@ -22,7 +22,6 @@ PASSES = K // (P * PACK)
 CHUNK = 128
 CHUNKS = S // CHUNK
 HALF = T // 2
-SCALAR_SHARE = (64, 40)
 PAIRED = 448
 
 
@@ -34,22 +33,20 @@ def tile_picked_zmae_mlprelu_po_kernel(
         keep = ctx.enter_context(tc.tile_pool(name="keep", bufs=1))
         psum = ctx.enter_context(tc.psum_pool(name="psum", bufs=1))
 
-        def sb(name, shape, dtype, tag=""):
+        shared = ctx.enter_context(tc.tile_pool(name="shared", bufs=1))
+
+        def sb(name, shape, dtype, tag="", offset=None):
+            if offset is not None:
+                return shared.tile(shape, dtype, name=name, tag=name, align_bytes=64, offset=offset)
             return keep.tile(shape, dtype, name=name, tag=tag or name, align_bytes=64)
 
         offsets = sb("offsets", [P, S // 16], U16)
-        nc.sync.dma_start(offsets[:], offs)
 
         xs_table = sb("xs_table", [P, T], U8)
         nc.vector.memset(xs_table[:].bitcast(I32), 0)
         w2s_raw = sb("w2s_raw", [P, N], U8)
-        nc.gpsimd.memset(w2s_raw[:].bitcast(I32), 0)
-        for q in range(4):
-            nc.gpsimd.dma_start(
-                w2s_raw[32 * q : 32 * q + 4, :].bitcast(I32), w2_scales[0, 4 * q : 4 * q + 4, :].bitcast(I32)
-            )
+        nc.vector.memset(w2s_raw[:].bitcast(I32), 0)
         w2w_raw = sb("w2w_raw", [P, 2 * N], U8)
-        nc.sync.dma_start(w2w_raw[:].bitcast(I32), w2_words[0].bitcast(I32))
 
         w1_rows = w1.rearrange("(g p j) c -> g p j c", g=PASSES, j=PACK)
         w1_raw = [sb("w1_raw%d" % g, [P, PACK, H], F32) for g in range(PASSES)]
@@ -64,6 +61,7 @@ def tile_picked_zmae_mlprelu_po_kernel(
             )
 
         load_x(0)
+        nc.sync.dma_start(offsets[:], offs)
         for q in range(4):
             nc.sync.dma_start(
                 xs_table[32 * q : 32 * q + 4 * PASSES, :].bitcast(I32),
@@ -72,6 +70,11 @@ def tile_picked_zmae_mlprelu_po_kernel(
         load_w1(0)
         load_w1(1)
         load_x(1)
+        for q in range(4):
+            nc.sync.dma_start(
+                w2s_raw[32 * q : 32 * q + 4, :].bitcast(I32), w2_scales[0, 4 * q : 4 * q + 4, :].bitcast(I32)
+            )
+        nc.sync.dma_start(w2w_raw[:].bitcast(I32), w2_words[0].bitcast(I32))
         mask_rows = mask.rearrange("(p t) c -> t p c", t=PACK)
         out_rows = out_0.rearrange("(p t) c -> t p c", t=PACK)
 
@@ -85,41 +88,51 @@ def tile_picked_zmae_mlprelu_po_kernel(
         w1_scales = [sb("w1_scales%d" % g, [P, H], U8) for g in range(PASSES)]
 
         def round_w1(g):
-            grouped = sb("w1_grouped%d" % g, [P, PACK * H], BF16, tag="w1_grouped")
-            dst = grouped[:].rearrange("p (t m j) -> p m j t", t=PACK, j=PACK)
+            halves = [
+                sb("w1_half%d_%d" % (g, u), [P, 2 * PACK * P], BF16, offset=0 if (g, u) == (1, 1) else None)
+                for u in range(2)
+            ]
             src = w1_raw[g][:].rearrange("p j (m t) -> p m j t", t=PACK)
-            cut = SCALAR_SHARE[g]
-            nc.scalar.activation(dst[:, :cut], src[:, :cut], COPY)
-            nc.vector.tensor_copy(dst[:, cut:], src[:, cut:])
-            return grouped
+            dst = [half[:].rearrange("p (t m j) -> p m j t", t=2, j=PACK) for half in halves]
+            nc.vector.tensor_copy(dst[0], src[:, :, :, 0:2])
+            nc.scalar.activation(dst[1], src[:, :, :, 2:4], COPY)
+            return halves
 
-        def quantise_w1(g, t0, t1, grouped):
+        def quantise_w1(g, u, halves):
             nc.vector.quantize_mx(
-                out=w1_codes[g][:, t0 * P : t1 * P].bitcast(FP8X4),
-                scales=w1_scales[g][:, t0 * P : t1 * P],
-                in_=grouped[:, t0 * PACK * P : t1 * PACK * P],
+                out=w1_codes[g][:, 2 * u * P : 2 * (u + 1) * P].bitcast(FP8X4),
+                scales=w1_scales[g][:, 2 * u * P : 2 * (u + 1) * P],
+                in_=halves[u][:],
             )
 
         def gather_x1(dst, first, last):
             nc.vector.tensor_copy(dst, x_table[1][:].indirect(entries(first, last)))
 
-        w2_codes = sb("w2_codes", [P, 2 * N], U8)
-        nc.vector.tensor_copy(
-            w2_codes[:].rearrange("p (t m b) -> p m t b", t=PACK, b=2),
-            w2w_raw[:].rearrange("p (m t b) -> p m t b", t=PACK, b=2),
-        )
         xs = sb("xs", [P, S], U8)
         xq0 = sb("xq0", [P, S], U32)
         nc.vector.tensor_copy(xq0[:], x_table[0][:].indirect(offsets[:]))
         nc.vector.tensor_copy(xs[:], xs_table[:].indirect(offsets[:]))
-        quantise_w1(0, 0, PACK, round_w1(0))
-        grouped = round_w1(1)
-        xq1 = [sb("xq1_early", [P, S // 2], U32, tag="w1_raw1")]
-        quantise_w1(1, 0, 1, grouped)
-        gather_x1(xq1[0][:, cols(0, 1)], 0, 1)
-        quantise_w1(1, 1, 2, grouped)
-        quantise_w1(1, 2, 4, grouped)
-        gather_x1(xq1[0][:, cols(1, 2)], 1, 2)
+        halves = round_w1(0)
+        quantise_w1(0, 0, halves)
+        quantise_w1(0, 1, halves)
+        halves = round_w1(1)
+        quantise_w1(1, 0, halves)
+        xq1 = {0: sb("xq1_0", [P, CHUNK], U32)}
+        gather_x1(xq1[0][:], 0, 1)
+        quantise_w1(1, 1, halves)
+        xq1[1] = sb("xq1_1", [P, CHUNK], U32, offset=0)
+        gather_x1(xq1[1][:], 1, 2)
+        w2_codes = sb("w2_codes", [P, 2 * N], U8, offset=N)
+        nc.vector.tensor_copy(
+            w2_codes[:].rearrange("p (t m b) -> p m t b", t=PACK, b=2),
+            w2w_raw[:].rearrange("p (m t b) -> p m t b", t=PACK, b=2),
+        )
+
+        w2_scale = sb("w2_scale", [P, N], U8, offset=3 * N)
+        nc.vector.tensor_copy(
+            w2_scale[:].rearrange("p (t m) -> p m t", t=PACK),
+            w2s_raw[:].rearrange("p (m t) -> p m t", t=PACK),
+        )
 
         window = []
 
@@ -127,7 +140,7 @@ def tile_picked_zmae_mlprelu_po_kernel(
             window.append(sb("window%d" % t, [P, T], F32, tag=tag))
             nc.sync.dma_start(window[t][:], mask_rows[t])
 
-        load_window(0, "w2w_raw")
+        load_window(0, "xs_table")
         load_window(1, "w1_raw0")
 
         parts = ((0, 1), (1, 2), (2, 4))
@@ -138,7 +151,7 @@ def tile_picked_zmae_mlprelu_po_kernel(
         def first_layer(c, t0, t1, tag, on_vector=False):
             acc = psum.tile([P, t1 - t0, CHUNK], F32, name="acc", tag=tag)
             span = cols(c, c + 1)
-            moving = (xq0[:, span], xq1[c // 2][:, cols(c % 2, c % 2 + 1)])
+            moving = (xq0[:, span], xq1[c][:] if c < 2 else xq1[2][:, cols(c - 2, c - 1)])
             for t in range(t0, t1):
                 for g in range(PASSES):
                     nc.tensor.matmul_mx(
@@ -190,29 +203,26 @@ def tile_picked_zmae_mlprelu_po_kernel(
         def scatter(t, first, last, values):
             nc.vector.tensor_copy(window[t][:].indirect(entries(first, last)), values)
 
-        w2_scale = sb("w2_scale", [P, N], U8, tag="w1_grouped")
-        nc.vector.tensor_copy(
-            w2_scale[:].rearrange("p (t m) -> p m t", t=PACK),
-            w2s_raw[:].rearrange("p (m t) -> p m t", t=PACK),
-        )
-        load_window(2, "w2s_raw")
         first_layer(0, 0, 2, "bank0")
         first_layer(0, 2, 4, "bank1")
-        quantise_h(0)
-        xq1.append(sb("xq1_late", [P, S // 2], U32, tag="h0"))
-        gather_x1(xq1[1][:], 2, 4)
+        load_window(2, "xq1_0")
+        quantise_h(0, tag="w2w_raw")
+        xq1[2] = sb("xq1_2", [P, 2 * CHUNK], U32, tag="h0")
+        gather_x1(xq1[2][:, cols(0, 1)], 2, 3)
+        gather_x1(xq1[2][:, cols(1, 2)], 3, 4)
         y00 = second_layer(0, 1, 0, 1, "bank3")
         y10 = second_layer(1, 2, 0, 1, "bank4")
-        first_layer(1, 0, 4, "bank2")
-        quantise_h(1)
+        first_layer(1, 0, 2, "bank2")
+        first_layer(1, 2, 4, "bank5")
+        quantise_h(1, tag="x_table1")
         scatter(0, 0, 1, y00[:, 0, :])
         scatter(1, 0, 1, y10[:, 0, :])
         first_layer(2, 0, 4, "bank0")
         load_window(3, "h1")
         y01 = second_layer(0, 2, 1, 2, "bank0")
-        first_layer(3, 0, 4, "bank1")
+        first_layer(3, 0, 4, "bank3")
         scatter(0, 1, 2, y01[:, 0, :])
-        quantise_h(2, tag="y1_0")
+        quantise_h(2, tag="y0_0")
         scatter(1, 1, 2, y01[:, 1, :])
         y02 = second_layer(0, 1, 2, 3, "bank6")
         scatter(0, 2, 4, y02[:, 0, :])

@@ -115,6 +115,30 @@ def tile_picked_zmae_mlprelu_po_kernel(
         halves = round_w1(0)
         quantise_w1(0, 0, halves)
         quantise_w1(0, 1, halves)
+
+        def first_passes(acc, g, c, t0, t1, moving):
+            for t in range(t0, t1):
+                nc.tensor.matmul_mx(
+                    out=acc[:, t - t0, :],
+                    lhsT=w1_codes[g][:, t * P : (t + 1) * P].bitcast(FP8X4),
+                    lhsT_scale=w1_scales[g][:, t * P : (t + 1) * P],
+                    rhs=moving.bitcast(FP8X4),
+                    rhs_scale=xs[4 * g :, cols(c, c + 1)],
+                    start=(g == 0 and t == t0),
+                    stop=(g == PASSES - 1 and t == t1 - 1),
+                )
+
+        sums = {}
+        for c, t0, t1, tag in (
+            (0, 0, 2, "bank0"),
+            (1, 0, 2, "bank2"),
+            (0, 2, 4, "bank1"),
+            (1, 2, 4, "bank5"),
+            (2, 0, 4, "bank6"),
+            (3, 0, 4, "bank7"),
+        ):
+            sums[c, t0] = psum.tile([P, t1 - t0, CHUNK], F32, name="acc", tag=tag)
+            first_passes(sums[c, t0], 0, c, t0, t1, xq0[:, cols(c, c + 1)])
         halves = round_w1(1)
         quantise_w1(1, 0, halves)
         xq1 = {0: sb("xq1_0", [P, CHUNK], U32)}
@@ -148,27 +172,12 @@ def tile_picked_zmae_mlprelu_po_kernel(
         h_codes = [sb("h_codes%d" % u, [P, (last - first) * CHUNK], U32) for u, (first, last) in enumerate(parts)]
         h_scales = []
 
-        def first_layer(c, t0, t1, tag, on_vector=False):
-            acc = psum.tile([P, t1 - t0, CHUNK], F32, name="acc", tag=tag)
-            span = cols(c, c + 1)
-            moving = (xq0[:, span], xq1[c][:] if c < 2 else xq1[2][:, cols(c - 2, c - 1)])
-            for t in range(t0, t1):
-                for g in range(PASSES):
-                    nc.tensor.matmul_mx(
-                        out=acc[:, t - t0, :],
-                        lhsT=w1_codes[g][:, t * P : (t + 1) * P].bitcast(FP8X4),
-                        lhsT_scale=w1_scales[g][:, t * P : (t + 1) * P],
-                        rhs=moving[g].bitcast(FP8X4),
-                        rhs_scale=xs[4 * g :, span],
-                        start=(g == 0),
-                        stop=(g == PASSES - 1),
-                    )
+        def first_layer(c, t0, t1):
+            acc = sums[c, t0]
+            first_passes(acc, 1, c, t0, t1, xq1[c][:] if c < 2 else xq1[2][:, cols(c - 2, c - 1)])
             dst = h[c][:] if c < 2 else h[2][:, cols(c - 2, c - 1), :]
             src = acc[:].rearrange("p t n -> p n t")
-            if on_vector:
-                nc.vector.tensor_scalar_max(dst[:, :, t0:t1], src, 0.0)
-            else:
-                nc.scalar.activation(dst[:, :, t0:t1], src, RELU)
+            nc.scalar.activation(dst[:, :, t0:t1], src, RELU)
 
         def quantise_h(u, tag=""):
             h_scales.append(sb("h_scales%d" % u, [P, (parts[u][1] - parts[u][0]) * CHUNK], U8, tag=tag))
@@ -203,8 +212,8 @@ def tile_picked_zmae_mlprelu_po_kernel(
         def scatter(t, first, last, values):
             nc.vector.tensor_copy(window[t][:].indirect(entries(first, last)), values)
 
-        first_layer(0, 0, 2, "bank0")
-        first_layer(0, 2, 4, "bank1")
+        first_layer(0, 0, 2)
+        first_layer(0, 2, 4)
         load_window(2, "xq1_0")
         quantise_h(0, tag="w2w_raw")
         xq1[2] = sb("xq1_2", [P, 2 * CHUNK], U32, tag="h0")
@@ -212,21 +221,21 @@ def tile_picked_zmae_mlprelu_po_kernel(
         gather_x1(xq1[2][:, cols(1, 2)], 3, 4)
         y00 = second_layer(0, 1, 0, 1, "bank3")
         y10 = second_layer(1, 2, 0, 1, "bank4")
-        first_layer(1, 0, 2, "bank2")
-        first_layer(1, 2, 4, "bank5")
+        first_layer(1, 0, 2)
+        first_layer(1, 2, 4)
         quantise_h(1, tag="x_table1")
         scatter(0, 0, 1, y00[:, 0, :])
         scatter(1, 0, 1, y10[:, 0, :])
-        first_layer(2, 0, 4, "bank0")
+        first_layer(2, 0, 4)
         load_window(3, "h1")
-        y01 = second_layer(0, 2, 1, 2, "bank0")
-        first_layer(3, 0, 4, "bank3")
+        y01 = second_layer(0, 2, 1, 2, "bank6")
+        first_layer(3, 0, 4)
         scatter(0, 1, 2, y01[:, 0, :])
         quantise_h(2, tag="y0_0")
         scatter(1, 1, 2, y01[:, 1, :])
-        y02 = second_layer(0, 1, 2, 3, "bank6")
+        y02 = second_layer(0, 1, 2, 3, "bank0")
         scatter(0, 2, 4, y02[:, 0, :])
-        y12 = second_layer(1, 2, 2, 3, "bank7")
+        y12 = second_layer(1, 2, 2, 3, "bank1")
         scatter(1, 2, 4, y12[:, 0, :])
         y_late = {t: second_layer(t, t + 1, 0, 3, "bank%d" % t) for t in (2, 3)}
 

@@ -21,8 +21,8 @@ PACK = 4
 PASSES = K // (P * PACK)
 CHUNK = 128
 CHUNKS = S // CHUNK
-HALF = T // 2
-PAIRED = 448
+QUARTER = T // 4
+FIRST_H = 4 * N
 
 
 def tile_picked_zmae_mlprelu_po_kernel(
@@ -131,9 +131,8 @@ def tile_picked_zmae_mlprelu_po_kernel(
         sums = {}
         for c, t0, t1, tag in (
             (0, 0, 2, "bank0"),
-            (1, 0, 2, "bank2"),
             (0, 2, 4, "bank1"),
-            (1, 2, 4, "bank5"),
+            (1, 0, 4, "bank2"),
             (2, 0, 4, "bank6"),
             (3, 0, 4, "bank7"),
         ):
@@ -168,7 +167,10 @@ def tile_picked_zmae_mlprelu_po_kernel(
         load_window(1, "w1_raw0")
 
         parts = ((0, 1), (1, 2), (2, 4))
-        h = [sb("h%d" % u, [P, (last - first) * CHUNK, PACK], BF16) for u, (first, last) in enumerate(parts)]
+        h = [
+            sb("h%d" % u, [P, (last - first) * CHUNK, PACK], BF16, offset=None if u else FIRST_H)
+            for u, (first, last) in enumerate(parts)
+        ]
         h_codes = [sb("h_codes%d" % u, [P, (last - first) * CHUNK], U32) for u, (first, last) in enumerate(parts)]
         h_scales = []
 
@@ -179,8 +181,8 @@ def tile_picked_zmae_mlprelu_po_kernel(
             src = acc[:].rearrange("p t n -> p n t")
             nc.scalar.activation(dst[:, :, t0:t1], src, RELU)
 
-        def quantise_h(u, tag=""):
-            h_scales.append(sb("h_scales%d" % u, [P, (parts[u][1] - parts[u][0]) * CHUNK], U8, tag=tag))
+        def quantise_h(u, tag="", offset=None):
+            h_scales.append(sb("h_scales%d" % u, [P, (parts[u][1] - parts[u][0]) * CHUNK], U8, tag=tag, offset=offset))
             nc.vector.quantize_mx(
                 out=h_codes[u][:].bitcast(FP8X4),
                 scales=h_scales[u][:],
@@ -214,59 +216,64 @@ def tile_picked_zmae_mlprelu_po_kernel(
 
         first_layer(0, 0, 2)
         first_layer(0, 2, 4)
-        load_window(2, "xq1_0")
+        load_window(2, "w1_raw1")
         quantise_h(0, tag="w2w_raw")
-        xq1[2] = sb("xq1_2", [P, 2 * CHUNK], U32, tag="h0")
+        xq1[2] = sb("xq1_2", [P, 2 * CHUNK], U32, offset=FIRST_H)
         gather_x1(xq1[2][:, cols(0, 1)], 2, 3)
         gather_x1(xq1[2][:, cols(1, 2)], 3, 4)
         y00 = second_layer(0, 1, 0, 1, "bank3")
-        y10 = second_layer(1, 2, 0, 1, "bank4")
-        first_layer(1, 0, 2)
-        first_layer(1, 2, 4)
-        quantise_h(1, tag="x_table1")
+        y10 = second_layer(1, 3, 0, 1, "bank4")
+        first_layer(1, 0, 4)
         scatter(0, 0, 1, y00[:, 0, :])
         scatter(1, 0, 1, y10[:, 0, :])
+        quantise_h(1, offset=FIRST_H)
+        scatter(2, 0, 1, y10[:, 1, :])
         first_layer(2, 0, 4)
         load_window(3, "h1")
-        y01 = second_layer(0, 2, 1, 2, "bank6")
         first_layer(3, 0, 4)
+        quantise_h(2)
+        y01 = second_layer(0, 2, 1, 2, "bank7")
         scatter(0, 1, 2, y01[:, 0, :])
-        quantise_h(2, tag="y0_0")
         scatter(1, 1, 2, y01[:, 1, :])
         y02 = second_layer(0, 1, 2, 3, "bank0")
         scatter(0, 2, 4, y02[:, 0, :])
         y12 = second_layer(1, 2, 2, 3, "bank1")
         scatter(1, 2, 4, y12[:, 0, :])
-        y_late = {t: second_layer(t, t + 1, 0, 3, "bank%d" % t) for t in (2, 3)}
+        y_late = {t: second_layer(t, t + 1, 3 - t, 3, "bank%d" % t) for t in (2, 3)}
 
-        pairs = sb("pairs", [P, 2, PAIRED, 2], BF16)
+        pair_row = sb("pairs", [P, 2 * 2 * QUARTER * 2], BF16)
+        both = pair_row[:].rearrange("p (h u c e) -> p h u c e", h=2, u=2, e=2)
+        pairs = [pair_row[:, h * T : (h + 1) * T] for h in range(2)]
         out_codes = sb("out_codes", [P, T], U32)
         out_scales = sb("out_scales", [P, T], U8)
         last = PACK - 1
-        spans = (slice(0, HALF), slice(HALF, HALF + T // 4), slice(HALF + T // 4, T))
-        rounded = [sb("rounded%d" % u, [P, span.stop - span.start, PACK], BF16) for u, span in enumerate(spans)]
-
-        def round_direct(t):
-            nc.scalar.activation(rounded[0][:, PAIRED:, t], window[t][:, PAIRED:HALF], COPY)
-            for u in (1, 2):
-                nc.scalar.activation(rounded[u][:, :, t], window[t][:, spans[u]], COPY)
+        spans = [slice(u * QUARTER, (u + 1) * QUARTER) for u in range(4)]
+        rounded = [sb("rounded%d" % u, [P, QUARTER, PACK], BF16) for u in range(4)]
 
         for t in range(PACK):
             if t > 1:
-                scatter(t, 0, CHUNKS, y_late[t][:, 0, :])
+                scatter(t, last - t, CHUNKS, y_late[t][:, 0, :])
             nc.sync.dma_start(out_rows[t], window[t][:])
             if t < last:
-                nc.scalar.activation(pairs[:, t // 2, :, t % 2], window[t][:, :PAIRED], COPY)
+                nc.scalar.activation(
+                    both[:, :, t // 2, :, t % 2],
+                    window[t][:, : 2 * QUARTER].rearrange("p (h c) -> p h c", h=2),
+                    COPY,
+                )
                 if t == last - 1:
-                    nc.scalar.activation(pairs[:, 1, 0, :], window[t][:, 0:1].to_broadcast([P, 2]), COPY)
+                    firsts = window[t][:, 0 : 2 * QUARTER : QUARTER].unsqueeze(2).to_broadcast([P, 2, 2])
+                    nc.scalar.activation(both[:, :, 1, 0, :], firsts, COPY)
             else:
-                nc.vector.tensor_copy(pairs[:, t // 2, :, t % 2], window[t][:, :PAIRED])
-            round_direct(t)
+                for u in (0, 1):
+                    nc.vector.tensor_copy(both[:, u, t // 2, :, t % 2], window[t][:, spans[u]])
+            for u in (2, 3):
+                nc.scalar.activation(rounded[u][:, :, t], window[t][:, spans[u]], COPY)
 
-        nc.vector.tensor_copy(
-            rounded[0][:, :PAIRED, :].bitcast(I32),
-            pairs[:].rearrange("p u c e -> p u (c e)").bitcast(I32).rearrange("p u c -> p c u"),
-        )
+        for u in (0, 1):
+            nc.vector.tensor_copy(
+                rounded[u][:].bitcast(I32),
+                pairs[u].bitcast(I32).rearrange("p (u c) -> p c u", u=2),
+            )
         words_out = out_1[0].rearrange("p c r -> p (c r)").bitcast(I32)
         for u, span in enumerate(spans):
             nc.vector.quantize_mx(
@@ -274,7 +281,9 @@ def tile_picked_zmae_mlprelu_po_kernel(
                 scales=out_scales[:, span],
                 in_=rounded[u][:].rearrange("p c t -> p (c t)"),
             )
-            nc.sync.dma_start(words_out[:, span], out_codes[:, span].bitcast(I32))
+            if u > 0:
+                done = slice(0 if u == 1 else span.start, span.stop)
+                nc.sync.dma_start(words_out[:, done], out_codes[:, done].bitcast(I32))
         for q in range(4):
             queue = nc.scalar if q % 2 else nc.sync
             queue.dma_start(

@@ -281,9 +281,7 @@ def tile_picked_zmae_mlprelu_po_kernel(
                 scales=out_scales[:, span],
                 in_=rounded[u][:].rearrange("p c t -> p (c t)"),
             )
-            if u > 0:
-                done = slice(0 if u == 1 else span.start, span.stop)
-                nc.sync.dma_start(words_out[:, done], out_codes[:, done].bitcast(I32))
+            nc.sync.dma_start(words_out[:, span], out_codes[:, span].bitcast(I32))
         for q in range(4):
             queue = nc.scalar if q % 2 else nc.sync
             queue.dma_start(

@@ -22,7 +22,7 @@ PASSES = K // (P * PACK)
 CHUNK = 128
 CHUNKS = S // CHUNK
 QUARTER = T // 4
-FIRST_H = 4 * N
+W2_BYTES = 4 * N
 
 
 def tile_picked_zmae_mlprelu_po_kernel(
@@ -46,7 +46,7 @@ def tile_picked_zmae_mlprelu_po_kernel(
         nc.vector.memset(xs_table[:].bitcast(I32), 0)
         w2s_raw = sb("w2s_raw", [P, N], U8)
         nc.vector.memset(w2s_raw[:].bitcast(I32), 0)
-        w2w_raw = sb("w2w_raw", [P, 2 * N], U8)
+        w2w_raw = sb("w2w_raw", [P, 2 * N], U8, offset=W2_BYTES)
 
         w1_rows = w1.rearrange("(g p j) c -> g p j c", g=PASSES, j=PACK)
         w1_raw = [sb("w1_raw%d" % g, [P, PACK, H], F32) for g in range(PASSES)]
@@ -167,10 +167,7 @@ def tile_picked_zmae_mlprelu_po_kernel(
         load_window(1, "w1_raw0")
 
         parts = ((0, 1), (1, 2), (2, 4))
-        h = [
-            sb("h%d" % u, [P, (last - first) * CHUNK, PACK], BF16, offset=None if u else FIRST_H)
-            for u, (first, last) in enumerate(parts)
-        ]
+        h = [sb("h%d" % u, [P, (last - first) * CHUNK, PACK], BF16) for u, (first, last) in enumerate(parts)]
         h_codes = [sb("h_codes%d" % u, [P, (last - first) * CHUNK], U32) for u, (first, last) in enumerate(parts)]
         h_scales = []
 
@@ -217,8 +214,8 @@ def tile_picked_zmae_mlprelu_po_kernel(
         first_layer(0, 0, 2)
         first_layer(0, 2, 4)
         load_window(2, "w1_raw1")
-        quantise_h(0, tag="w2w_raw")
-        xq1[2] = sb("xq1_2", [P, 2 * CHUNK], U32, offset=FIRST_H)
+        quantise_h(0, offset=W2_BYTES)
+        xq1[2] = sb("xq1_2", [P, 2 * CHUNK], U32, offset=W2_BYTES + CHUNK)
         gather_x1(xq1[2][:, cols(0, 1)], 2, 3)
         gather_x1(xq1[2][:, cols(1, 2)], 3, 4)
         y00 = second_layer(0, 1, 0, 1, "bank3")
@@ -226,7 +223,7 @@ def tile_picked_zmae_mlprelu_po_kernel(
         first_layer(1, 0, 4)
         scatter(0, 0, 1, y00[:, 0, :])
         scatter(1, 0, 1, y10[:, 0, :])
-        quantise_h(1, offset=FIRST_H)
+        quantise_h(1, offset=W2_BYTES + CHUNK)
         scatter(2, 0, 1, y10[:, 1, :])
         first_layer(2, 0, 4)
         load_window(3, "h1")

@@ -278,9 +278,10 @@ def tile_picked_zmae_mlprelu_po_kernel(
                 scales=out_scales[:, span],
                 in_=rounded[u][:].rearrange("p c t -> p (c t)"),
             )
-            nc.sync.dma_start(words_out[:, span], out_codes[:, span].bitcast(I32))
+            queue = nc.scalar if u % 2 else nc.sync
+            queue.dma_start(words_out[:, span], out_codes[:, span].bitcast(I32))
         for q in range(4):
-            queue = nc.scalar if q % 2 else nc.sync
+            queue = nc.scalar if q == 3 else nc.sync
             queue.dma_start(
                 out_2[0, 4 * q : 4 * q + 4, :].bitcast(I32), out_scales[32 * q : 32 * q + 4, :].bitcast(I32)
             )

@@ -15,6 +15,7 @@ FP8X4 = mybir.dt.float8_e4m3fn_x4
 FP4X4 = mybir.dt.float4_e2m1fn_x4
 RELU = mybir.ActivationFunctionType.Relu
 COPY = mybir.ActivationFunctionType.Copy
+ADD = mybir.AluOpType.add
 
 P = 128
 PACK = 4
@@ -23,6 +24,11 @@ CHUNK = 128
 CHUNKS = S // CHUNK
 QUARTER = T // 4
 W2_BYTES = 4 * N
+HALF = CHUNK // 2
+AHEAD = 3
+H_BYTES = 4096
+Y_BYTES = 8192
+HALF_BYTES = 12288
 
 
 def tile_picked_zmae_mlprelu_po_kernel(
@@ -44,7 +50,7 @@ def tile_picked_zmae_mlprelu_po_kernel(
 
         xs_table = sb("xs_table", [P, T], U8)
         nc.vector.memset(xs_table[:].bitcast(I32), 0)
-        w2s_raw = sb("w2s_raw", [P, N], U8)
+        w2s_raw = sb("w2s_raw", [P, N], U8, offset=0)
         nc.vector.memset(w2s_raw[:].bitcast(I32), 0)
         w2w_raw = sb("w2w_raw", [P, 2 * N], U8, offset=W2_BYTES)
 
@@ -89,7 +95,7 @@ def tile_picked_zmae_mlprelu_po_kernel(
 
         def round_w1(g):
             halves = [
-                sb("w1_half%d_%d" % (g, u), [P, 2 * PACK * P], BF16, offset=0 if (g, u) == (1, 1) else None)
+                sb("w1_half%d_%d" % (g, u), [P, 2 * PACK * P], BF16, offset=HALF_BYTES if (g, u) == (1, 1) else None)
                 for u in range(2)
             ]
             src = w1_raw[g][:].rearrange("p j (m t) -> p m j t", t=PACK)
@@ -129,127 +135,147 @@ def tile_picked_zmae_mlprelu_po_kernel(
                 )
 
         sums = {}
-        for c, t0, t1, tag in (
-            (0, 0, 2, "bank0"),
-            (0, 2, 4, "bank1"),
-            (1, 0, 4, "bank2"),
-            (2, 0, 4, "bank6"),
-            (3, 0, 4, "bank7"),
-        ):
-            sums[c, t0] = psum.tile([P, t1 - t0, CHUNK], F32, name="acc", tag=tag)
-            first_passes(sums[c, t0], 0, c, t0, t1, xq0[:, cols(c, c + 1)])
+        for c in range(CHUNKS):
+            sums[c] = psum.tile([P, PACK, CHUNK], F32, name="acc", tag="bank%d" % c)
+            first_passes(sums[c], 0, c, 0, PACK, xq0[:, cols(c, c + 1)])
         halves = round_w1(1)
         quantise_w1(1, 0, halves)
         xq1 = {0: sb("xq1_0", [P, CHUNK], U32)}
         gather_x1(xq1[0][:], 0, 1)
         quantise_w1(1, 1, halves)
-        xq1[1] = sb("xq1_1", [P, CHUNK], U32, offset=0)
+        xq1[1] = sb("xq1_1", [P, CHUNK], U32, offset=HALF_BYTES)
         gather_x1(xq1[1][:], 1, 2)
-        w2_codes = sb("w2_codes", [P, 2 * N], U8, offset=N)
+        w2_codes = sb("w2_codes", [P, 2 * N], U8)
         nc.vector.tensor_copy(
-            w2_codes[:].rearrange("p (t m b) -> p m t b", t=PACK, b=2),
-            w2w_raw[:].rearrange("p (m t b) -> p m t b", t=PACK, b=2),
+            w2_codes[:].bitcast(U16).rearrange("p (t m) -> p m t", t=PACK),
+            w2w_raw[:].bitcast(U16).rearrange("p (m t) -> p m t", t=PACK),
         )
 
-        w2_scale = sb("w2_scale", [P, N], U8, offset=3 * N)
-        nc.vector.tensor_copy(
-            w2_scale[:].rearrange("p (t m) -> p m t", t=PACK),
-            w2s_raw[:].rearrange("p (m t) -> p m t", t=PACK),
-        )
+        scale_slots = w2s_raw[:].rearrange("p (m t) -> p m t", t=PACK)
+        early_scale = sb("early_scale", [P, 2, P], U8)
+        nc.vector.tensor_copy(early_scale[:].rearrange("p t m -> p m t"), scale_slots[:, :, 0:2])
+        w2_scale = {t: early_scale[:, t, :] for t in range(2)}
 
         window = []
 
-        def load_window(t, tag):
+        def load_window(t, tag, queue=nc.sync):
             window.append(sb("window%d" % t, [P, T], F32, tag=tag))
-            nc.sync.dma_start(window[t][:], mask_rows[t])
+            queue.dma_start(window[t][:], mask_rows[t])
 
         load_window(0, "xs_table")
-        load_window(1, "w1_raw0")
+        load_window(1, "w1_raw1", nc.scalar)
 
-        parts = ((0, 1), (1, 2), (2, 4))
-        h = [sb("h%d" % u, [P, (last - first) * CHUNK, PACK], BF16) for u, (first, last) in enumerate(parts)]
-        h_codes = [sb("h_codes%d" % u, [P, (last - first) * CHUNK], U32) for u, (first, last) in enumerate(parts)]
-        h_scales = []
+        h = sb("h", [P, S * PACK], BF16, offset=H_BYTES)
+        first_codes = sb("first_codes", [P, CHUNK], U32)
+        zeros = sb("zeros", [P, HALF], F32)
+        nc.vector.memset(first_codes[:].bitcast(I32), 0)
+        nc.vector.memset(zeros[:], 0.0)
+        codes = {
+            0: sb("codes0", [P, CHUNK], U32),
+            1: sb("codes1", [P, CHUNK], U32),
+            2: sb("codes2", [P, 2 * CHUNK], U32),
+            AHEAD: first_codes,
+        }
+        scales = {}
 
-        def first_layer(c, t0, t1):
-            acc = sums[c, t0]
-            first_passes(acc, 1, c, t0, t1, xq1[c][:] if c < 2 else xq1[2][:, cols(c - 2, c - 1)])
-            dst = h[c][:] if c < 2 else h[2][:, cols(c - 2, c - 1), :]
-            src = acc[:].rearrange("p t n -> p n t")
-            nc.scalar.activation(dst[:, :, t0:t1], src, RELU)
+        def relu(c, e0, e1):
+            dst = h[:, (c * CHUNK + e0) * PACK : (c * CHUNK + e1) * PACK].rearrange("p (n t) -> p n t", t=PACK)
+            nc.scalar.activation(dst, sums[c][:, :, e0:e1].rearrange("p t n -> p n t"), RELU)
 
-        def quantise_h(u, tag="", offset=None):
-            h_scales.append(sb("h_scales%d" % u, [P, (parts[u][1] - parts[u][0]) * CHUNK], U8, tag=tag, offset=offset))
+        def quantise_h(part, e0, e1):
+            base = 0 if part == AHEAD else part * CHUNK
             nc.vector.quantize_mx(
-                out=h_codes[u][:].bitcast(FP8X4),
-                scales=h_scales[u][:],
-                in_=h[u][:].rearrange("p n t -> p (n t)"),
+                out=codes[part][:, e0:e1].bitcast(FP8X4),
+                scales=scales[part][:, e0:e1],
+                in_=h[:, (base + e0) * PACK : (base + e1) * PACK],
             )
 
-        def second_layer(t0, t1, u0, u1, tag, on_vector=False):
-            first, last = parts[u0][0], parts[u1 - 1][1]
-            width = (last - first) * CHUNK
-            acc = psum.tile([P, t1 - t0, width], F32, name="acc", tag=tag)
-            for t in range(t0, t1):
-                for u in range(u0, u1):
+        def second_layer(name, slots, parts, e0, e1, tag, offset=None):
+            widths = [codes[part].shape[1] for part in parts]
+            acc = psum.tile([P, len(slots), sum(widths)], F32, name="acc", tag=tag)
+            for i, t in enumerate(slots):
+                for k, part in enumerate(parts):
                     nc.tensor.matmul_mx(
-                        out=acc[:, t - t0, cols(parts[u][0] - first, parts[u][1] - first)],
+                        out=acc[:, i, sum(widths[:k]) : sum(widths[: k + 1])],
                         lhsT=w2_codes[:, 2 * t * P : 2 * (t + 1) * P].bitcast(FP4X4),
-                        lhsT_scale=w2_scale[:, t * P : (t + 1) * P],
-                        rhs=h_codes[u][:].bitcast(FP8X4),
-                        rhs_scale=h_scales[u][:],
+                        lhsT_scale=w2_scale[t],
+                        rhs=codes[part][:].bitcast(FP8X4),
+                        rhs_scale=scales[part][:],
                         start=True,
                         stop=True,
                     )
-            y = sb("y%d_%d" % (t0, u0), [P, t1 - t0, width], F32)
-            if on_vector:
-                nc.vector.tensor_copy(y[:], acc[:])
-            else:
-                nc.scalar.activation(y[:], acc[:], COPY)
+            y = sb(name, [P, len(slots), e1 - e0], F32, offset=offset)
+            nc.scalar.activation(y[:], acc[:, :, e0:e1], COPY)
             return y
 
-        def scatter(t, first, last, values):
-            nc.vector.tensor_copy(window[t][:].indirect(entries(first, last)), values)
+        def scatter(t, e0, e1, values):
+            target = window[t][:].indirect(offsets[:, e0 // 16 : e1 // 16])
+            if e1 - e0 == HALF:
+                nc.vector.tensor_tensor(target, values, zeros[:], ADD)
+            else:
+                nc.vector.tensor_copy(target, values)
 
-        first_layer(0, 0, 2)
-        first_layer(0, 2, 4)
-        load_window(2, "w1_raw1")
-        quantise_h(0, offset=W2_BYTES)
-        xq1[2] = sb("xq1_2", [P, 2 * CHUNK], U32, offset=W2_BYTES + CHUNK)
-        gather_x1(xq1[2][:, cols(0, 1)], 2, 3)
-        gather_x1(xq1[2][:, cols(1, 2)], 3, 4)
-        y00 = second_layer(0, 1, 0, 1, "bank3")
-        y10 = second_layer(1, 3, 0, 1, "bank4")
-        first_layer(1, 0, 4)
-        scatter(0, 0, 1, y00[:, 0, :])
-        scatter(1, 0, 1, y10[:, 0, :])
-        quantise_h(1, offset=W2_BYTES + CHUNK)
-        scatter(2, 0, 1, y10[:, 1, :])
-        first_layer(2, 0, 4)
-        load_window(3, "h1")
-        first_layer(3, 0, 4)
-        quantise_h(2)
-        y01 = second_layer(0, 2, 1, 2, "bank7")
-        scatter(0, 1, 2, y01[:, 0, :])
-        scatter(1, 1, 2, y01[:, 1, :])
-        y02 = second_layer(0, 1, 2, 3, "bank0")
-        scatter(0, 2, 4, y02[:, 0, :])
-        y12 = second_layer(1, 2, 2, 3, "bank1")
-        scatter(1, 2, 4, y12[:, 0, :])
-        y_late = {t: second_layer(t, t + 1, 3 - t, 3, "bank%d" % t) for t in (2, 3)}
+        first_passes(sums[0], 1, 0, 0, PACK, xq1[0][:])
+        relu(0, 0, HALF)
+        relu(0, HALF, CHUNK)
+        first_passes(sums[1], 1, 1, 0, PACK, xq1[1][:])
+        relu(1, 0, CHUNK)
+        load_window(2, "xq0")
+        scales[AHEAD] = sb("scales_ahead", [P, CHUNK], U8, offset=W2_BYTES)
+        nc.vector.memset(scales[AHEAD][:, HALF:].bitcast(I32), 0)
+        quantise_h(AHEAD, 0, HALF)
+        for c in (2, 3):
+            xq1[c] = sb("xq1_%d" % c, [P, CHUNK], U32, offset=W2_BYTES + (4 * c - 5) * CHUNK)
+            gather_x1(xq1[c][:], c, c + 1)
+            if c == 2:
+                scales[0] = sb("scales0", [P, CHUNK], U8, offset=W2_BYTES + CHUNK)
+                quantise_h(0, 0, CHUNK)
+        ya = [
+            second_layer("ya%d" % t, (t,), (AHEAD,), 0, HALF, "bank%d" % (4 + t), Y_BYTES + 256 * t) for t in range(2)
+        ]
+        scales[1] = sb("scales1", [P, CHUNK], U8, offset=W2_BYTES + 2 * CHUNK)
+        quantise_h(1, 0, CHUNK)
+        for t in range(2):
+            scatter(t, 0, HALF, ya[t][:, 0, :])
+        yb = [
+            second_layer("yb%d" % t, (t,), (0,), HALF, CHUNK, "bank%d" % (6 + t), Y_BYTES + 1024 + 256 * t)
+            for t in range(2)
+        ]
+        first_passes(sums[2], 1, 2, 0, PACK, xq1[2][:])
+        relu(2, 0, CHUNK)
+        first_passes(sums[3], 1, 3, 0, PACK, xq1[3][:])
+        relu(3, 0, CHUNK)
+        yc0 = second_layer("yc0", (0,), (1,), 0, CHUNK, "bank4")
+        load_window(3, "xq1_0")
+        for t in range(2):
+            scatter(t, HALF, CHUNK, yb[t][:, 0, :])
+        scales[2] = sb("scales2", [P, 2 * CHUNK], U8, offset=Y_BYTES + 1024)
+        quantise_h(2, 0, 2 * CHUNK)
+        yc1 = second_layer("yc1", (1,), (1,), 0, CHUNK, "bank6", H_BYTES)
+        late_scale = sb("late_scale", [P, 2, P], U8, offset=H_BYTES + 1024)
+        nc.gpsimd.tensor_copy(late_scale[:], scale_slots[:, :, 2:4].rearrange("p m t -> p t m"))
+        for t in (2, 3):
+            w2_scale[t] = late_scale[:, t - 2, :]
+        scatter(0, CHUNK, 2 * CHUNK, yc0[:, 0, :])
+        scatter(1, CHUNK, 2 * CHUNK, yc1[:, 0, :])
+        for t in range(2):
+            yd = second_layer("yd%d" % t, (t,), (2,), 0, 2 * CHUNK, "bank%d" % (4 + t))
+            scatter(t, 2 * CHUNK, S, yd[:, 0, :])
+        y_late = {t: second_layer("ye%d" % t, (t,), (0, 1, 2), 0, S, "bank%d" % t) for t in (2, 3)}
 
         pair_row = sb("pairs", [P, 2 * 2 * QUARTER * 2], BF16)
         both = pair_row[:].rearrange("p (h u c e) -> p h u c e", h=2, u=2, e=2)
         pairs = [pair_row[:, h * T : (h + 1) * T] for h in range(2)]
-        out_codes = sb("out_codes", [P, T], U32)
         out_scales = sb("out_scales", [P, T], U8)
         last = PACK - 1
-        spans = [slice(u * QUARTER, (u + 1) * QUARTER) for u in range(4)]
-        rounded = [sb("rounded%d" % u, [P, QUARTER, PACK], BF16) for u in range(4)]
+        edges = [0, QUARTER, 2 * QUARTER, 2 * QUARTER + CHUNK, T - CHUNK, T]
+        spans = [slice(edges[u], edges[u + 1]) for u in range(5)]
+        rounded = [sb("rounded%d" % u, [P, edges[u + 1] - edges[u], PACK], BF16) for u in range(5)]
+        out_codes = [sb("out_codes%d" % u, [P, edges[u + 1] - edges[u]], U32) for u in range(5)]
 
         for t in range(PACK):
             if t > 1:
-                scatter(t, last - t, CHUNKS, y_late[t][:, 0, :])
+                scatter(t, 0, S, y_late[t][:, 0, :])
             nc.sync.dma_start(out_rows[t], window[t][:])
             if t < last:
                 nc.scalar.activation(
@@ -263,23 +289,32 @@ def tile_picked_zmae_mlprelu_po_kernel(
             else:
                 for u in (0, 1):
                     nc.vector.tensor_copy(both[:, u, t // 2, :, t % 2], window[t][:, spans[u]])
-            for u in (2, 3):
+            for u in (2, 3, 4):
                 nc.scalar.activation(rounded[u][:, :, t], window[t][:, spans[u]], COPY)
 
-        for u in (0, 1):
+        words_out = out_1[0].rearrange("p c r -> p (c r)").bitcast(I32)
+
+        def merge(u):
             nc.vector.tensor_copy(
                 rounded[u][:].bitcast(I32),
                 pairs[u].bitcast(I32).rearrange("p (u c) -> p c u", u=2),
             )
-        words_out = out_1[0].rearrange("p c r -> p (c r)").bitcast(I32)
-        for u, span in enumerate(spans):
+
+        def finish(u, queue):
             nc.vector.quantize_mx(
-                out=out_codes[:, span].bitcast(FP8X4),
-                scales=out_scales[:, span],
+                out=out_codes[u][:].bitcast(FP8X4),
+                scales=out_scales[:, spans[u]],
                 in_=rounded[u][:].rearrange("p c t -> p (c t)"),
             )
-            queue = nc.scalar if u % 2 else nc.sync
-            queue.dma_start(words_out[:, span], out_codes[:, span].bitcast(I32))
+            queue.dma_start(words_out[:, spans[u]], out_codes[u][:].bitcast(I32))
+
+        merge(0)
+        finish(2, nc.sync)
+        merge(1)
+        finish(0, nc.sync)
+        finish(1, nc.sync)
+        finish(3, nc.scalar)
+        finish(4, nc.scalar)
         for q in range(4):
             queue = nc.scalar if q == 3 else nc.sync
             queue.dma_start(

@@ -152,8 +152,8 @@ def tile_picked_zmae_mlprelu_po_kernel(
         )
 
         scale_slots = w2s_raw[:].rearrange("p (m t) -> p m t", t=PACK)
-        early_scale = sb("early_scale", [P, 2, P], U8)
-        nc.vector.tensor_copy(early_scale[:].rearrange("p t m -> p m t"), scale_slots[:, :, 0:2])
+        early_scale = sb("early_scale", [P, 2, P], U8, offset=HALF_BYTES + 1024)
+        nc.gpsimd.tensor_copy(early_scale[:], scale_slots[:, :, 0:2].rearrange("p m t -> p t m"))
         w2_scale = {t: early_scale[:, t, :] for t in range(2)}
 
         window = []
@@ -222,7 +222,7 @@ def tile_picked_zmae_mlprelu_po_kernel(
         relu(1, 0, CHUNK)
         load_window(2, "xq0")
         scales[AHEAD] = sb("scales_ahead", [P, CHUNK], U8, offset=W2_BYTES)
-        nc.vector.memset(scales[AHEAD][:, HALF:].bitcast(I32), 0)
+        nc.gpsimd.memset(scales[AHEAD][:, HALF:].bitcast(I32), 0)
         quantise_h(AHEAD, 0, HALF)
         for c in (2, 3):
             xq1[c] = sb("xq1_%d" % c, [P, CHUNK], U32, offset=W2_BYTES + (4 * c - 5) * CHUNK)

@@ -16,19 +16,16 @@ FP4X4 = mybir.dt.float4_e2m1fn_x4
 RELU = mybir.ActivationFunctionType.Relu
 COPY = mybir.ActivationFunctionType.Copy
 ADD = mybir.AluOpType.add
+MULT = mybir.AluOpType.mult
 
 P = 128
 PACK = 4
 PASSES = K // (P * PACK)
 CHUNK = 128
 CHUNKS = S // CHUNK
-QUARTER = T // 4
-W2_BYTES = 4 * N
-HALF = CHUNK // 2
-AHEAD = 3
-H_BYTES = 4096
-Y_BYTES = 8192
-HALF_BYTES = 12288
+HALF = S // 2
+PIECE = T // 4
+HANDED = 128
 
 
 def tile_picked_zmae_mlprelu_po_kernel(
@@ -39,27 +36,21 @@ def tile_picked_zmae_mlprelu_po_kernel(
         keep = ctx.enter_context(tc.tile_pool(name="keep", bufs=1))
         psum = ctx.enter_context(tc.psum_pool(name="psum", bufs=1))
 
-        shared = ctx.enter_context(tc.tile_pool(name="shared", bufs=1))
-
-        def sb(name, shape, dtype, tag="", offset=None):
-            if offset is not None:
-                return shared.tile(shape, dtype, name=name, tag=name, align_bytes=64, offset=offset)
+        def sb(name, shape, dtype, tag=""):
             return keep.tile(shape, dtype, name=name, tag=tag or name, align_bytes=64)
 
         offsets = sb("offsets", [P, S // 16], U16)
-
         xs_table = sb("xs_table", [P, T], U8)
         nc.vector.memset(xs_table[:].bitcast(I32), 0)
-        w2s_raw = sb("w2s_raw", [P, N], U8, offset=0)
+        w2s_raw = sb("w2s_raw", [P, N], U8)
         nc.vector.memset(w2s_raw[:].bitcast(I32), 0)
-        w2w_raw = sb("w2w_raw", [P, 2 * N], U8, offset=W2_BYTES)
+        w2w_raw = sb("w2w_raw", [P, 2 * N], U8)
 
         w1_rows = w1.rearrange("(g p j) c -> g p j c", g=PASSES, j=PACK)
         w1_raw = [sb("w1_raw%d" % g, [P, PACK, H], F32) for g in range(PASSES)]
         x_table = [sb("x_table%d" % g, [P, T], U32) for g in range(PASSES)]
-
-        def load_w1(g):
-            nc.sync.dma_start(w1_raw[g][:], w1_rows[g])
+        mask_rows = mask.rearrange("(p t) c -> t p c", t=PACK)
+        out_rows = out_0.rearrange("(p t) c -> t p c", t=PACK)
 
         def load_x(g):
             nc.sync.dma_start(
@@ -73,31 +64,26 @@ def tile_picked_zmae_mlprelu_po_kernel(
                 xs_table[32 * q : 32 * q + 4 * PASSES, :].bitcast(I32),
                 x_scales[:, 4 * q : 4 * q + 4, :].bitcast(I32),
             )
-        load_w1(0)
-        load_w1(1)
+        for g in range(PASSES):
+            nc.sync.dma_start(w1_raw[g][:], w1_rows[g])
         load_x(1)
+        nc.sync.dma_start(w2w_raw[:].bitcast(I32), w2_words[0].bitcast(I32))
         for q in range(4):
             nc.sync.dma_start(
                 w2s_raw[32 * q : 32 * q + 4, :].bitcast(I32), w2_scales[0, 4 * q : 4 * q + 4, :].bitcast(I32)
             )
-        nc.sync.dma_start(w2w_raw[:].bitcast(I32), w2_words[0].bitcast(I32))
-        mask_rows = mask.rearrange("(p t) c -> t p c", t=PACK)
-        out_rows = out_0.rearrange("(p t) c -> t p c", t=PACK)
-
-        def cols(first, last):
-            return slice(first * CHUNK, last * CHUNK)
+        window = [sb("window%d" % t, [P, T], F32) for t in range(PACK)]
+        for t in (0, 1, 3, 2):
+            nc.sync.dma_start(window[t][:], mask_rows[t])
 
         def entries(first, last):
-            return offsets[:, first * CHUNK // 16 : last * CHUNK // 16]
+            return offsets[:, first // 16 : last // 16]
 
         w1_codes = [sb("w1_codes%d" % g, [P, H], U32) for g in range(PASSES)]
         w1_scales = [sb("w1_scales%d" % g, [P, H], U8) for g in range(PASSES)]
 
         def round_w1(g):
-            halves = [
-                sb("w1_half%d_%d" % (g, u), [P, 2 * PACK * P], BF16, offset=HALF_BYTES if (g, u) == (1, 1) else None)
-                for u in range(2)
-            ]
+            halves = [sb("w1_half%d_%d" % (g, u), [P, 2 * PACK * P], BF16) for u in range(2)]
             src = w1_raw[g][:].rearrange("p j (m t) -> p m j t", t=PACK)
             dst = [half[:].rearrange("p (t m j) -> p m j t", t=2, j=PACK) for half in halves]
             nc.vector.tensor_copy(dst[0], src[:, :, :, 0:2])
@@ -111,9 +97,6 @@ def tile_picked_zmae_mlprelu_po_kernel(
                 in_=halves[u][:],
             )
 
-        def gather_x1(dst, first, last):
-            nc.vector.tensor_copy(dst, x_table[1][:].indirect(entries(first, last)))
-
         xs = sb("xs", [P, S], U8)
         xq0 = sb("xq0", [P, S], U32)
         nc.vector.tensor_copy(xq0[:], x_table[0][:].indirect(offsets[:]))
@@ -122,199 +105,163 @@ def tile_picked_zmae_mlprelu_po_kernel(
         quantise_w1(0, 0, halves)
         quantise_w1(0, 1, halves)
 
-        def first_passes(acc, g, c, t0, t1, moving):
-            for t in range(t0, t1):
+        def first_passes(g, c, moving):
+            for t in range(PACK):
                 nc.tensor.matmul_mx(
-                    out=acc[:, t - t0, :],
+                    out=sums[c][:, t, :],
                     lhsT=w1_codes[g][:, t * P : (t + 1) * P].bitcast(FP8X4),
                     lhsT_scale=w1_scales[g][:, t * P : (t + 1) * P],
                     rhs=moving.bitcast(FP8X4),
-                    rhs_scale=xs[4 * g :, cols(c, c + 1)],
-                    start=(g == 0 and t == t0),
-                    stop=(g == PASSES - 1 and t == t1 - 1),
+                    rhs_scale=xs[4 * g :, c * CHUNK : (c + 1) * CHUNK],
+                    start=(g == 0 and t == 0),
+                    stop=(g == PASSES - 1 and t == PACK - 1),
                 )
 
-        sums = {}
+        sums = [psum.tile([P, PACK, CHUNK], F32, name="acc", tag="bank%d" % c) for c in range(CHUNKS)]
         for c in range(CHUNKS):
-            sums[c] = psum.tile([P, PACK, CHUNK], F32, name="acc", tag="bank%d" % c)
-            first_passes(sums[c], 0, c, 0, PACK, xq0[:, cols(c, c + 1)])
+            first_passes(0, c, xq0[:, c * CHUNK : (c + 1) * CHUNK])
+
+        def gather_x1(name, first, last):
+            picked = sb(name, [P, last - first], U32)
+            nc.vector.tensor_copy(picked[:], x_table[1][:].indirect(entries(first, last)))
+            return picked
+
         halves = round_w1(1)
         quantise_w1(1, 0, halves)
-        xq1 = {0: sb("xq1_0", [P, CHUNK], U32)}
-        gather_x1(xq1[0][:], 0, 1)
+        xq1_0 = gather_x1("xq1_0", 0, CHUNK)
         quantise_w1(1, 1, halves)
-        xq1[1] = sb("xq1_1", [P, CHUNK], U32, offset=HALF_BYTES)
-        gather_x1(xq1[1][:], 1, 2)
+        xq1_1 = gather_x1("xq1_1", CHUNK, HALF)
+        xq1_b = gather_x1("xq1_b", HALF, S)
+
         w2_codes = sb("w2_codes", [P, 2 * N], U8)
-        nc.vector.tensor_copy(
+        nc.scalar.copy(
             w2_codes[:].bitcast(U16).rearrange("p (t m) -> p m t", t=PACK),
             w2w_raw[:].bitcast(U16).rearrange("p (m t) -> p m t", t=PACK),
         )
+        scale_slots = w2s_raw[:].rearrange("p (m t) -> p t m", t=PACK)
+        early_scale = sb("early_scale", [P, 2, P], U8, tag="w1_half1_1")
+        nc.gpsimd.tensor_copy(early_scale[:], scale_slots[:, 0:2, :])
 
-        scale_slots = w2s_raw[:].rearrange("p (m t) -> p m t", t=PACK)
-        early_scale = sb("early_scale", [P, 2, P], U8, offset=HALF_BYTES + 1024)
-        nc.gpsimd.tensor_copy(early_scale[:], scale_slots[:, :, 0:2].rearrange("p m t -> p t m"))
-        w2_scale = {t: early_scale[:, t, :] for t in range(2)}
+        h = [sb("h0", [P, HALF * PACK], BF16), sb("h1", [P, HALF * PACK], BF16, tag="w2w_raw")]
+        h_codes = sb("h_codes", [P, S], U32)
+        h_scales = sb("h_scales", [P, S], U8)
 
-        window = []
+        def relu(c, on_vector=False):
+            dst = h[c // 2][:, (c % 2) * CHUNK * PACK : (c % 2 + 1) * CHUNK * PACK]
+            dst = dst.rearrange("p (n t) -> p n t", t=PACK)
+            src = sums[c][:].rearrange("p t n -> p n t")
+            if on_vector:
+                nc.vector.tensor_scalar_max(dst, src, 0.0)
+            else:
+                nc.scalar.activation(dst, src, RELU)
 
-        def load_window(t, tag, queue=nc.sync):
-            window.append(sb("window%d" % t, [P, T], F32, tag=tag))
-            queue.dma_start(window[t][:], mask_rows[t])
-
-        load_window(0, "xs_table")
-        load_window(1, "w1_raw1", nc.scalar)
-
-        h = sb("h", [P, S * PACK], BF16, offset=H_BYTES)
-        first_codes = sb("first_codes", [P, CHUNK], U32)
-        zeros = sb("zeros", [P, HALF], F32)
-        nc.vector.memset(first_codes[:].bitcast(I32), 0)
-        nc.vector.memset(zeros[:], 0.0)
-        codes = {
-            0: sb("codes0", [P, CHUNK], U32),
-            1: sb("codes1", [P, CHUNK], U32),
-            2: sb("codes2", [P, 2 * CHUNK], U32),
-            AHEAD: first_codes,
-        }
-        scales = {}
-
-        def relu(c, e0, e1):
-            dst = h[:, (c * CHUNK + e0) * PACK : (c * CHUNK + e1) * PACK].rearrange("p (n t) -> p n t", t=PACK)
-            nc.scalar.activation(dst, sums[c][:, :, e0:e1].rearrange("p t n -> p n t"), RELU)
-
-        def quantise_h(part, e0, e1):
-            base = 0 if part == AHEAD else part * CHUNK
+        def quantise_h(u):
             nc.vector.quantize_mx(
-                out=codes[part][:, e0:e1].bitcast(FP8X4),
-                scales=scales[part][:, e0:e1],
-                in_=h[:, (base + e0) * PACK : (base + e1) * PACK],
+                out=h_codes[:, u * HALF : (u + 1) * HALF].bitcast(FP8X4),
+                scales=h_scales[:, u * HALF : (u + 1) * HALF],
+                in_=h[u][:],
             )
 
-        def second_layer(name, slots, parts, e0, e1, tag, offset=None):
-            widths = [codes[part].shape[1] for part in parts]
-            acc = psum.tile([P, len(slots), sum(widths)], F32, name="acc", tag=tag)
-            for i, t in enumerate(slots):
-                for k, part in enumerate(parts):
-                    nc.tensor.matmul_mx(
-                        out=acc[:, i, sum(widths[:k]) : sum(widths[: k + 1])],
-                        lhsT=w2_codes[:, 2 * t * P : 2 * (t + 1) * P].bitcast(FP4X4),
-                        lhsT_scale=w2_scale[t],
-                        rhs=codes[part][:].bitcast(FP8X4),
-                        rhs_scale=scales[part][:],
-                        start=True,
-                        stop=True,
-                    )
-            y = sb(name, [P, len(slots), e1 - e0], F32, offset=offset)
-            nc.scalar.activation(y[:], acc[:, :, e0:e1], COPY)
+        def second_layer(t, scale, first, last, bank):
+            acc = psum.tile([P, last - first], F32, name="acc", tag="bank%d" % bank)
+            nc.tensor.matmul_mx(
+                out=acc[:],
+                lhsT=w2_codes[:, 2 * t * P : 2 * (t + 1) * P].bitcast(FP4X4),
+                lhsT_scale=scale,
+                rhs=h_codes[:, first:last].bitcast(FP8X4),
+                rhs_scale=h_scales[:, first:last],
+                start=True,
+                stop=True,
+            )
+            return acc
+
+        def leave_bank(name, acc, on_vector, tag=""):
+            y = sb(name, [P, acc.shape[1]], F32, tag=tag)
+            if on_vector:
+                nc.vector.tensor_copy(y[:], acc)
+            else:
+                nc.scalar.activation(y[:], acc, COPY)
             return y
 
-        def scatter(t, e0, e1, values):
-            target = window[t][:].indirect(offsets[:, e0 // 16 : e1 // 16])
-            if e1 - e0 == HALF:
-                nc.vector.tensor_tensor(target, values, zeros[:], ADD)
-            else:
+        def scatter(t, first, last, values, on_vector):
+            target = window[t][:].indirect(entries(first, last))
+            if on_vector:
                 nc.vector.tensor_copy(target, values)
-
-        first_passes(sums[0], 1, 0, 0, PACK, xq1[0][:])
-        relu(0, 0, HALF)
-        relu(0, HALF, CHUNK)
-        first_passes(sums[1], 1, 1, 0, PACK, xq1[1][:])
-        relu(1, 0, CHUNK)
-        load_window(2, "xq0")
-        scales[AHEAD] = sb("scales_ahead", [P, CHUNK], U8, offset=W2_BYTES)
-        nc.gpsimd.memset(scales[AHEAD][:, HALF:].bitcast(I32), 0)
-        quantise_h(AHEAD, 0, HALF)
-        for c in (2, 3):
-            xq1[c] = sb("xq1_%d" % c, [P, CHUNK], U32, offset=W2_BYTES + (4 * c - 5) * CHUNK)
-            gather_x1(xq1[c][:], c, c + 1)
-            if c == 2:
-                scales[0] = sb("scales0", [P, CHUNK], U8, offset=W2_BYTES + CHUNK)
-                quantise_h(0, 0, CHUNK)
-        ya = [
-            second_layer("ya%d" % t, (t,), (AHEAD,), 0, HALF, "bank%d" % (4 + t), Y_BYTES + 256 * t) for t in range(2)
-        ]
-        scales[1] = sb("scales1", [P, CHUNK], U8, offset=W2_BYTES + 2 * CHUNK)
-        quantise_h(1, 0, CHUNK)
-        for t in range(2):
-            scatter(t, 0, HALF, ya[t][:, 0, :])
-        yb = [
-            second_layer("yb%d" % t, (t,), (0,), HALF, CHUNK, "bank%d" % (6 + t), Y_BYTES + 1024 + 256 * t)
-            for t in range(2)
-        ]
-        first_passes(sums[2], 1, 2, 0, PACK, xq1[2][:])
-        relu(2, 0, CHUNK)
-        first_passes(sums[3], 1, 3, 0, PACK, xq1[3][:])
-        relu(3, 0, CHUNK)
-        yc0 = second_layer("yc0", (0,), (1,), 0, CHUNK, "bank4")
-        load_window(3, "xq1_0")
-        for t in range(2):
-            scatter(t, HALF, CHUNK, yb[t][:, 0, :])
-        scales[2] = sb("scales2", [P, 2 * CHUNK], U8, offset=Y_BYTES + 1024)
-        quantise_h(2, 0, 2 * CHUNK)
-        yc1 = second_layer("yc1", (1,), (1,), 0, CHUNK, "bank6", H_BYTES)
-        late_scale = sb("late_scale", [P, 2, P], U8, offset=H_BYTES + 1024)
-        nc.gpsimd.tensor_copy(late_scale[:], scale_slots[:, :, 2:4].rearrange("p m t -> p t m"))
-        for t in (2, 3):
-            w2_scale[t] = late_scale[:, t - 2, :]
-        scatter(0, CHUNK, 2 * CHUNK, yc0[:, 0, :])
-        scatter(1, CHUNK, 2 * CHUNK, yc1[:, 0, :])
-        for t in range(2):
-            yd = second_layer("yd%d" % t, (t,), (2,), 0, 2 * CHUNK, "bank%d" % (4 + t))
-            scatter(t, 2 * CHUNK, S, yd[:, 0, :])
-        y_late = {t: second_layer("ye%d" % t, (t,), (0, 1, 2), 0, S, "bank%d" % t) for t in (2, 3)}
-
-        pair_row = sb("pairs", [P, 2 * 2 * QUARTER * 2], BF16)
-        both = pair_row[:].rearrange("p (h u c e) -> p h u c e", h=2, u=2, e=2)
-        pairs = [pair_row[:, h * T : (h + 1) * T] for h in range(2)]
-        out_scales = sb("out_scales", [P, T], U8)
-        last = PACK - 1
-        edges = [0, QUARTER, 2 * QUARTER, 2 * QUARTER + CHUNK, T - CHUNK, T]
-        spans = [slice(edges[u], edges[u + 1]) for u in range(5)]
-        rounded = [sb("rounded%d" % u, [P, edges[u + 1] - edges[u], PACK], BF16) for u in range(5)]
-        out_codes = [sb("out_codes%d" % u, [P, edges[u + 1] - edges[u]], U32) for u in range(5)]
-
-        for t in range(PACK):
-            if t > 1:
-                scatter(t, 0, S, y_late[t][:, 0, :])
-            nc.sync.dma_start(out_rows[t], window[t][:])
-            if t < last:
-                nc.scalar.activation(
-                    both[:, :, t // 2, :, t % 2],
-                    window[t][:, : 2 * QUARTER].rearrange("p (h c) -> p h c", h=2),
-                    COPY,
-                )
-                if t == last - 1:
-                    firsts = window[t][:, 0 : 2 * QUARTER : QUARTER].unsqueeze(2).to_broadcast([P, 2, 2])
-                    nc.scalar.activation(both[:, :, 1, 0, :], firsts, COPY)
             else:
-                for u in (0, 1):
-                    nc.vector.tensor_copy(both[:, u, t // 2, :, t % 2], window[t][:, spans[u]])
-            for u in (2, 3, 4):
-                nc.scalar.activation(rounded[u][:, :, t], window[t][:, spans[u]], COPY)
+                nc.scalar.activation(target, values, COPY)
 
+        first_passes(1, 0, xq1_0[:])
+        relu(0)
+        first_passes(1, 1, xq1_1[:])
+        relu(1, on_vector=True)
+        for c in (2, 3):
+            first_passes(1, c, xq1_b[:, (c - 2) * CHUNK : (c - 1) * CHUNK])
+        relu(2)
+        quantise_h(0)
+        relu(3)
+        acc_a = [second_layer(t, early_scale[:, t, :], 0, HALF, 4 + t) for t in range(2)]
+        y_a = [leave_bank("y_a%d" % t, acc_a[t][:], t == 0) for t in range(2)]
+        quantise_h(1)
+        late_scale = sb("late_scale", [P, 2, P], U8, tag="w2w_raw")
+        nc.gpsimd.tensor_copy(late_scale[:], scale_slots[:, 2:4, :])
+        acc_b = [second_layer(t, early_scale[:, t, :], HALF, S, 6 + t) for t in range(2)]
+        acc_late = {t: second_layer(t, late_scale[:, t - 2, :], 0, S, t - 2) for t in (2, 3)}
+        for t in range(2):
+            scatter(t, 0, HALF, y_a[t][:], t == 0)
+        y_b = [leave_bank("y_b%d" % t, acc_b[t][:], t == 0) for t in range(2)]
+        y2 = leave_bank("y2", acc_late[2][:], False)
+        for t in range(2):
+            scatter(t, HALF, S, y_b[t][:], t == 0)
+        y3_first = leave_bank("y3_first", acc_late[3][:, : S - HANDED], False)
+        scatter(2, 0, S, y2[:], True)
+        scatter(3, 0, S - HANDED, y3_first[:], False)
+        y3_last = leave_bank("y3_last", acc_late[3][:, S - HANDED :], True, tag="y2")
+
+        pair_rows = [sb("pairs%d" % side, [P, 2 * 2 * PIECE * 2], BF16) for side in range(2)]
+        pairs = [row[:].rearrange("p (h u c e) -> p h u c e", h=2, u=2, e=2) for row in pair_rows]
+
+        def columns(t, side):
+            return window[t][:, side * 2 * PIECE : (side + 1) * 2 * PIECE].rearrange("p (h c) -> p h c", h=2)
+
+        for t in range(2):
+            nc.sync.dma_start(out_rows[t], window[t][:])
+            for side in range(2):
+                nc.gpsimd.tensor_scalar(pairs[side][:, :, 0, :, t], columns(t, side), 1.0, -0.0, MULT, ADD)
+        nc.sync.dma_start(out_rows[2], window[2][:])
+        nc.vector.tensor_copy(pairs[0][:, :, 1, :, 0], columns(2, 0))
+        nc.scalar.activation(pairs[1][:, :, 1, :, 0], columns(2, 1), COPY)
+        scatter(3, S - HANDED, S, y3_last[:], True)
+        nc.sync.dma_start(out_rows[3], window[3][:])
+
+        rounded = [sb("rounded%d" % u, [P, PIECE, PACK], BF16) for u in range(4)]
+        out_codes = [sb("out_codes%d" % u, [P, PIECE], U32) for u in range(4)]
+        out_scales = sb("out_scales", [P, T], U8)
         words_out = out_1[0].rearrange("p c r -> p (c r)").bitcast(I32)
 
         def merge(u):
-            nc.vector.tensor_copy(
-                rounded[u][:].bitcast(I32),
-                pairs[u].bitcast(I32).rearrange("p (u c) -> p c u", u=2),
-            )
+            src = pair_rows[u // 2][:, (u % 2) * T : (u % 2 + 1) * T]
+            if u < 2:
+                nc.vector.tensor_copy(
+                    rounded[u][:].bitcast(I32), src.bitcast(I32).rearrange("p (u c) -> p c u", u=2)
+                )
+            else:
+                nc.scalar.copy(rounded[u][:].bitcast(U32), src.bitcast(U32).rearrange("p (u c) -> p c u", u=2))
 
-        def finish(u, queue):
+        for half in range(2):
+            nc.vector.tensor_copy(pairs[0][:, half, 1, :, 1], columns(3, 0)[:, half, :])
+        for half in range(2):
+            nc.scalar.activation(pairs[1][:, half, 1, :, 1], columns(3, 1)[:, half, :], COPY)
+        for u in range(4):
+            merge(u)
+        for u in range(4):
+            span = slice(u * PIECE, (u + 1) * PIECE)
             nc.vector.quantize_mx(
                 out=out_codes[u][:].bitcast(FP8X4),
-                scales=out_scales[:, spans[u]],
+                scales=out_scales[:, span],
                 in_=rounded[u][:].rearrange("p c t -> p (c t)"),
             )
-            queue.dma_start(words_out[:, spans[u]], out_codes[u][:].bitcast(I32))
-
-        merge(0)
-        finish(2, nc.sync)
-        merge(1)
-        finish(0, nc.sync)
-        finish(1, nc.sync)
-        finish(3, nc.scalar)
-        finish(4, nc.scalar)
+            queue = nc.sync if u < 2 else nc.scalar
+            queue.dma_start(words_out[:, span], out_codes[u][:].bitcast(I32))
         for q in range(4):
             queue = nc.scalar if q == 3 else nc.sync
             queue.dma_start(

from contextlib import ExitStack

import concourse.mybir as mybir

K, T, S, H, N = 1024, 1024, 512, 512, 512
FLOPS = 2 * K * H * S + 2 * H * N * S

F32 = mybir.dt.float32
BF16 = mybir.dt.bfloat16
I32 = mybir.dt.int32
U32 = mybir.dt.uint32
U16 = mybir.dt.uint16
U8 = mybir.dt.uint8
FP8X4 = mybir.dt.float8_e4m3fn_x4
FP4X4 = mybir.dt.float4_e2m1fn_x4
RELU = mybir.ActivationFunctionType.Relu
COPY = mybir.ActivationFunctionType.Copy
ADD = mybir.AluOpType.add
MULT = mybir.AluOpType.mult

P = 128
PACK = 4
PASSES = K // (P * PACK)
CHUNK = 128
CHUNKS = S // CHUNK
HALF = S // 2
PIECE = T // 4
HANDED = 128


def tile_picked_zmae_mlprelu_po_kernel(
    tc, x_words, x_scales, mask, w1, w2_words, w2_scales, offs, out_0, out_1, out_2
):
    nc = tc.nc
    with ExitStack() as ctx:
        keep = ctx.enter_context(tc.tile_pool(name="keep", bufs=1))
        psum = ctx.enter_context(tc.psum_pool(name="psum", bufs=1))

        def sb(name, shape, dtype, tag=""):
            return keep.tile(shape, dtype, name=name, tag=tag or name, align_bytes=64)

        offsets = sb("offsets", [P, S // 16], U16)
        xs_table = sb("xs_table", [P, T], U8)
        nc.vector.memset(xs_table[:].bitcast(I32), 0)
        w2s_raw = sb("w2s_raw", [P, N], U8)
        nc.vector.memset(w2s_raw[:].bitcast(I32), 0)
        w2w_raw = sb("w2w_raw", [P, 2 * N], U8)

        w1_rows = w1.rearrange("(g p j) c -> g p j c", g=PASSES, j=PACK)
        w1_raw = [sb("w1_raw%d" % g, [P, PACK, H], F32) for g in range(PASSES)]
        x_table = [sb("x_table%d" % g, [P, T], U32) for g in range(PASSES)]
        mask_rows = mask.rearrange("(p t) c -> t p c", t=PACK)
        out_rows = out_0.rearrange("(p t) c -> t p c", t=PACK)

        def load_x(g):
            nc.sync.dma_start(
                x_table[g][:].bitcast(I32), x_words[g].rearrange("p c r -> p (c r)").bitcast(I32)
            )

        load_x(0)
        nc.sync.dma_start(offsets[:], offs)
        for q in range(4):
            nc.sync.dma_start(
                xs_table[32 * q : 32 * q + 4 * PASSES, :].bitcast(I32),
                x_scales[:, 4 * q : 4 * q + 4, :].bitcast(I32),
            )
        for g in range(PASSES):
            nc.sync.dma_start(w1_raw[g][:], w1_rows[g])
        load_x(1)
        nc.sync.dma_start(w2w_raw[:].bitcast(I32), w2_words[0].bitcast(I32))
        for q in range(4):
            nc.sync.dma_start(
                w2s_raw[32 * q : 32 * q + 4, :].bitcast(I32), w2_scales[0, 4 * q : 4 * q + 4, :].bitcast(I32)
            )
        window = [sb("window%d" % t, [P, T], F32) for t in range(PACK)]
        for t in (0, 1, 3, 2):
            nc.sync.dma_start(window[t][:], mask_rows[t])

        def entries(first, last):
            return offsets[:, first // 16 : last // 16]

        w1_codes = [sb("w1_codes%d" % g, [P, H], U32) for g in range(PASSES)]
        w1_scales = [sb("w1_scales%d" % g, [P, H], U8) for g in range(PASSES)]

        def round_w1(g):
            halves = [sb("w1_half%d_%d" % (g, u), [P, 2 * PACK * P], BF16) for u in range(2)]
            src = w1_raw[g][:].rearrange("p j (m t) -> p m j t", t=PACK)
            dst = [half[:].rearrange("p (t m j) -> p m j t", t=2, j=PACK) for half in halves]
            nc.vector.tensor_copy(dst[0], src[:, :, :, 0:2])
            nc.scalar.activation(dst[1], src[:, :, :, 2:4], COPY)
            return halves

        def quantise_w1(g, u, halves):
            nc.vector.quantize_mx(
                out=w1_codes[g][:, 2 * u * P : 2 * (u + 1) * P].bitcast(FP8X4),
                scales=w1_scales[g][:, 2 * u * P : 2 * (u + 1) * P],
                in_=halves[u][:],
            )

        xs = sb("xs", [P, S], U8)
        xq0 = sb("xq0", [P, S], U32)
        nc.vector.tensor_copy(xq0[:], x_table[0][:].indirect(offsets[:]))
        nc.vector.tensor_copy(xs[:], xs_table[:].indirect(offsets[:]))
        halves = round_w1(0)
        quantise_w1(0, 0, halves)
        quantise_w1(0, 1, halves)

        def first_passes(g, c, moving):
            for t in range(PACK):
                nc.tensor.matmul_mx(
                    out=sums[c][:, t, :],
                    lhsT=w1_codes[g][:, t * P : (t + 1) * P].bitcast(FP8X4),
                    lhsT_scale=w1_scales[g][:, t * P : (t + 1) * P],
                    rhs=moving.bitcast(FP8X4),
                    rhs_scale=xs[4 * g :, c * CHUNK : (c + 1) * CHUNK],
                    start=(g == 0 and t == 0),
                    stop=(g == PASSES - 1 and t == PACK - 1),
                )

        sums = [psum.tile([P, PACK, CHUNK], F32, name="acc", tag="bank%d" % c) for c in range(CHUNKS)]
        for c in range(CHUNKS):
            first_passes(0, c, xq0[:, c * CHUNK : (c + 1) * CHUNK])

        def gather_x1(name, first, last):
            picked = sb(name, [P, last - first], U32)
            nc.vector.tensor_copy(picked[:], x_table[1][:].indirect(entries(first, last)))
            return picked

        halves = round_w1(1)
        quantise_w1(1, 0, halves)
        xq1_0 = gather_x1("xq1_0", 0, CHUNK)
        quantise_w1(1, 1, halves)
        xq1_1 = gather_x1("xq1_1", CHUNK, HALF)
        xq1_b = gather_x1("xq1_b", HALF, S)

        w2_codes = sb("w2_codes", [P, 2 * N], U8)
        nc.scalar.copy(
            w2_codes[:].bitcast(U16).rearrange("p (t m) -> p m t", t=PACK),
            w2w_raw[:].bitcast(U16).rearrange("p (m t) -> p m t", t=PACK),
        )
        scale_slots = w2s_raw[:].rearrange("p (m t) -> p t m", t=PACK)
        early_scale = sb("early_scale", [P, 2, P], U8, tag="w1_half1_1")
        nc.gpsimd.tensor_copy(early_scale[:], scale_slots[:, 0:2, :])

        h = [sb("h0", [P, HALF * PACK], BF16), sb("h1", [P, HALF * PACK], BF16, tag="w2w_raw")]
        h_codes = sb("h_codes", [P, S], U32)
        h_scales = sb("h_scales", [P, S], U8)

        def relu(c, on_vector=False):
            dst = h[c // 2][:, (c % 2) * CHUNK * PACK : (c % 2 + 1) * CHUNK * PACK]
            dst = dst.rearrange("p (n t) -> p n t", t=PACK)
            src = sums[c][:].rearrange("p t n -> p n t")
            if on_vector:
                nc.vector.tensor_scalar_max(dst, src, 0.0)
            else:
                nc.scalar.activation(dst, src, RELU)

        def quantise_h(u):
            nc.vector.quantize_mx(
                out=h_codes[:, u * HALF : (u + 1) * HALF].bitcast(FP8X4),
                scales=h_scales[:, u * HALF : (u + 1) * HALF],
                in_=h[u][:],
            )

        def second_layer(t, scale, first, last, bank):
            acc = psum.tile([P, last - first], F32, name="acc", tag="bank%d" % bank)
            nc.tensor.matmul_mx(
                out=acc[:],
                lhsT=w2_codes[:, 2 * t * P : 2 * (t + 1) * P].bitcast(FP4X4),
                lhsT_scale=scale,
                rhs=h_codes[:, first:last].bitcast(FP8X4),
                rhs_scale=h_scales[:, first:last],
                start=True,
                stop=True,
            )
            return acc

        def leave_bank(name, acc, on_vector, tag=""):
            y = sb(name, [P, acc.shape[1]], F32, tag=tag)
            if on_vector:
                nc.vector.tensor_copy(y[:], acc)
            else:
                nc.scalar.activation(y[:], acc, COPY)
            return y

        def scatter(t, first, last, values, on_vector):
            target = window[t][:].indirect(entries(first, last))
            if on_vector:
                nc.vector.tensor_copy(target, values)
            else:
                nc.scalar.activation(target, values, COPY)

        first_passes(1, 0, xq1_0[:])
        relu(0)
        first_passes(1, 1, xq1_1[:])
        relu(1, on_vector=True)
        for c in (2, 3):
            first_passes(1, c, xq1_b[:, (c - 2) * CHUNK : (c - 1) * CHUNK])
        relu(2)
        quantise_h(0)
        relu(3)
        acc_a = [second_layer(t, early_scale[:, t, :], 0, HALF, 4 + t) for t in range(2)]
        y_a = [leave_bank("y_a%d" % t, acc_a[t][:], t == 0) for t in range(2)]
        quantise_h(1)
        late_scale = sb("late_scale", [P, 2, P], U8, tag="w2w_raw")
        nc.gpsimd.tensor_copy(late_scale[:], scale_slots[:, 2:4, :])
        acc_b = [second_layer(t, early_scale[:, t, :], HALF, S, 6 + t) for t in range(2)]
        acc_late = {t: second_layer(t, late_scale[:, t - 2, :], 0, S, t - 2) for t in (2, 3)}
        for t in range(2):
            scatter(t, 0, HALF, y_a[t][:], t == 0)
        y_b = [leave_bank("y_b%d" % t, acc_b[t][:], t == 0) for t in range(2)]
        y2 = leave_bank("y2", acc_late[2][:], False)
        for t in range(2):
            scatter(t, HALF, S, y_b[t][:], t == 0)
        y3_first = leave_bank("y3_first", acc_late[3][:, : S - HANDED], False)
        scatter(2, 0, S, y2[:], True)
        scatter(3, 0, S - HANDED, y3_first[:], False)
        y3_last = leave_bank("y3_last", acc_late[3][:, S - HANDED :], True, tag="y2")

        pair_rows = [sb("pairs%d" % side, [P, 2 * 2 * PIECE * 2], BF16) for side in range(2)]
        pairs = [row[:].rearrange("p (h u c e) -> p h u c e", h=2, u=2, e=2) for row in pair_rows]

        def columns(t, side):
            return window[t][:, side * 2 * PIECE : (side + 1) * 2 * PIECE].rearrange("p (h c) -> p h c", h=2)

        for t in range(2):
            nc.sync.dma_start(out_rows[t], window[t][:])
            for side in range(2):
                nc.gpsimd.tensor_scalar(pairs[side][:, :, 0, :, t], columns(t, side), 1.0, -0.0, MULT, ADD)
        nc.sync.dma_start(out_rows[2], window[2][:])
        nc.vector.tensor_copy(pairs[0][:, :, 1, :, 0], columns(2, 0))
        nc.scalar.activation(pairs[1][:, :, 1, :, 0], columns(2, 1), COPY)
        scatter(3, S - HANDED, S, y3_last[:], True)
        nc.sync.dma_start(out_rows[3], window[3][:])

        rounded = [sb("rounded%d" % u, [P, PIECE, PACK], BF16) for u in range(4)]
        out_codes = [sb("out_codes%d" % u, [P, PIECE], U32) for u in range(4)]
        out_scales = sb("out_scales", [P, T], U8)
        words_out = out_1[0].rearrange("p c r -> p (c r)").bitcast(I32)

        def merge(u):
            src = pair_rows[u // 2][:, (u % 2) * T : (u % 2 + 1) * T]
            if u < 2:
                nc.vector.tensor_copy(
                    rounded[u][:].bitcast(I32), src.bitcast(I32).rearrange("p (u c) -> p c u", u=2)
                )
            else:
                nc.scalar.copy(rounded[u][:].bitcast(U32), src.bitcast(U32).rearrange("p (u c) -> p c u", u=2))

        for half in range(2):
            nc.vector.tensor_copy(pairs[0][:, half, 1, :, 1], columns(3, 0)[:, half, :])
        for half in range(2):
            nc.scalar.activation(pairs[1][:, half, 1, :, 1], columns(3, 1)[:, half, :], COPY)
        for u in range(4):
            merge(u)
        for u in range(4):
            span = slice(u * PIECE, (u + 1) * PIECE)
            nc.vector.quantize_mx(
                out=out_codes[u][:].bitcast(FP8X4),
                scales=out_scales[:, span],
                in_=rounded[u][:].rearrange("p c t -> p (c t)"),
            )
            queue = nc.sync if u < 2 else nc.scalar
            queue.dma_start(words_out[:, span], out_codes[u][:].bitcast(I32))
        for q in range(4):
            queue = nc.scalar if q == 3 else nc.sync
            queue.dma_start(
                out_2[0, 4 * q : 4 * q + 4, :].bitcast(I32), out_scales[32 * q : 32 * q + 4, :].bitcast(I32)
            )
